import numpy as np
import ml_dtypes


def mxq(x, axis, fmt="e4m3"):
    dtype, down = {"e4m3": (ml_dtypes.float8_e4m3fn, 7), "e5m2": (ml_dtypes.float8_e5m2, 14)}[fmt]
    v = np.moveaxis(np.asarray(x, np.float32).astype(ml_dtypes.bfloat16).astype(np.float64), axis, -1)
    blocks = v.reshape(v.shape[:-1] + (-1, 32))
    amax = np.abs(blocks).max(-1, keepdims=True)
    byte = np.maximum(np.where(amax > 0, np.frexp(amax)[1] - 1 + 127, 0) - down, 1)
    scale = np.exp2(byte - 127.0)
    codes = (blocks / scale).astype(np.float32).astype(dtype).astype(np.float64)
    return np.moveaxis((codes * scale).reshape(v.shape), -1, axis)


WIDE = False


def mx_kscale(k):
    if not WIDE:
        return np.ones(k)
    levels = np.array([10, -10, 5, -5, 0])
    if k % 512:
        return np.exp2(np.random.permutation(np.resize(levels, k // 32))).repeat(32)
    a = np.empty((k // 512, 16))
    for p in range(k // 512):
        a[p, :8] = np.random.permutation(np.resize(levels, 8))
        for g in range(8):
            far = levels[np.abs(levels - a[p, g]) >= 10]
            a[p, g + 8] = far[np.random.randint(len(far))]
    return np.exp2(a.ravel()).repeat(32)


BF16 = ml_dtypes.bfloat16


def bf(x):
    return np.asarray(x, np.float32).astype(BF16)


def f64(x):
    return np.asarray(x).astype(np.float64)


M, N, K, D, R, Q = 1024, 1536, 1024, 512, 512, 512


def draw0():
    s, d = mx_kscale(K), mx_kscale(D)
    t, u = mx_kscale(N), mx_kscale(M)
    return {"fx": bf(np.random.standard_normal((M, K)) * s * u[:, None]),
            "fz": bf(np.random.standard_normal((K, N)) / np.sqrt(K) / s[:, None] * t),
            "gx": bf(0.5 * np.random.standard_normal((M, D)) * d),
            "gz": bf(np.random.standard_normal((D, N)) / np.sqrt(D) / d[:, None]),
            "amp_x": bf(0.2 * np.random.standard_normal(M)),
            "amp_z": bf(0.2 * np.random.standard_normal(N)),
            "alpha": bf(np.random.standard_normal((N, R)) / np.sqrt(N) / t[:, None]),
            "prior": bf(0.3 * np.random.standard_normal(R)),
            "scale_x": bf((1 + 0.1 * np.random.standard_normal(M)) / u),
            "v": bf(np.random.standard_normal((Q, M)) / np.sqrt(M) / u),
            "prec_z": bf((1 + 0.1 * np.random.standard_normal(N)) / t)}


def core(fx, fz, gx, gz, amp_x, amp_z, alpha, prior, scale_x, v, prec_z):
    lin = mxq(f64(fx), 1, "e4m3") @ mxq(f64(fz), 0, "e4m3")
    ex = mxq(f64(gx), 1, "e4m3") @ mxq(f64(gz), 0, "e4m3")
    c = lin * np.exp(ex + f64(amp_x)[:, None] + f64(amp_z))
    fit = mxq(c, 1, "e4m3") @ mxq(f64(alpha), 0, "e4m3")
    mean = f64(prior) + f64(scale_x)[:, None] * fit
    func = mxq(f64(v), 1, "e4m3") @ mxq(c, 0, "e4m3")
    cov = func * f64(prec_z)
    return mean, cov


def e4m3fn_bytes(y):
    return np.clip(np.asarray(y, np.float64), -448.0, 448.0).astype(np.float32).astype(ml_dtypes.float8_e4m3fn).view(np.uint8)


def e4m3fn_values(b):
    return np.asarray(b, np.uint8).view(ml_dtypes.float8_e4m3fn).astype(np.float64)


def setup_inputs():
    d = draw0()
    x0 = np.asarray(d['gz']).astype(np.float64)
    s = (np.max(np.abs(x0), axis=(1,), keepdims=True) / 448.0).astype(np.float32)
    out = {}
    for k, v in d.items():
        if k == 'gz':
            out['gz_bytes'] = e4m3fn_bytes(x0 / s.astype(np.float64))
            out['gz_scale'] = s
        else:
            out[k] = v
    return out


def reference(fx, fz, gx, gz_bytes, gz_scale, amp_x, amp_z, alpha, prior, scale_x, v, prec_z):
    return core(fx, fz, gx, e4m3fn_values(gz_bytes) * gz_scale.astype(np.float64), amp_x, amp_z, alpha, prior, scale_x, v, prec_z)

@@ -1,0 +1,579 @@
+from contextlib import ExitStack
+
+import concourse.mybir as mybir
+from concourse.masks import make_identity
+
+M, N, K, D, R, Q = 1024, 1536, 1024, 512, 512, 512
+FLOPS = 2 * M * N * (K + D + R + Q)
+
+F32 = mybir.dt.float32
+BF16 = mybir.dt.bfloat16
+U32 = mybir.dt.uint32
+I32 = mybir.dt.int32
+U8 = mybir.dt.uint8
+FP8 = mybir.dt.float8_e4m3fn
+FP8X4 = mybir.dt.float8_e4m3fn_x4
+ACT = mybir.ActivationFunctionType
+ALU = mybir.AluOpType
+
+P = 128
+B = 512
+
+
+SEQ = [
+    ("spread_az", 0),
+    ("load_gz", 1),
+    ("spread_az", 1),
+    ("load_gz", 0),
+    ("load_gx", 0, 0),
+    ("load_fz", 0, 0),
+    ("widen", 1, 1, "V"),
+    ("widen", 1, 2, "V"),
+    ("load_gx", 0, 1),
+    ("widen", 0, 1, "V"),
+    ("widen", 0, 3, "A"),
+    ("widen", 0, 0, "V"),
+    ("widen", 0, 2, "V"),
+    ("load_fz", 0, 1),
+    ("spread_az", 2),
+    ("widen", 1, 0, "V"),
+    ("load_fx", 0, 0),
+    ("lay_gz", 0, "V", 256, 512),
+    ("load_fx", 0, 1),
+    ("lay_fz", 0, 0, "V", 0, 256),
+    ("tr_gx", 0, 0, "V"),
+    ("load_fz", 1, 0),
+    ("lay_gz", 0, "A", 0, 256),
+    ("q_gz", 0),
+    ("lay_fz", 0, 0, "V", 256, 512),
+    ("tr_gx", 0, 1, "A"),
+    ("q_gx", 0),
+    ("q_fz", 0, 0),
+    ("lay_fz", 0, 1, "A", 0, 256),
+    ("tr_x", 0, 0, "A"),
+    ("lay_fz", 0, 1, "A", 256, 512),
+    ("front", 0),
+    ("load_gx", 1, 0),
+    ("widen", 1, 3, "A"),
+    ("lay_fz", 1, 0, "G", 0, 256),
+    ("lay_fz", 1, 0, "G", 256, 512),
+    ("tr_x", 0, 1, "V"),
+    ("front", 1),
+    ("load_fx", 1, 0),
+    ("lay_gz", 1, "A", 256, 512),
+    ("load_fx", 0, 3),
+    ("load_fz", 2, 0),
+    ("load_fx", 0, 2),
+    ("front", 3),
+    ("load_fz", 1, 1),
+    ("load_gz", 2),
+    ("tr_x", 0, 3, "V"),
+    ("q_fx", 0, 0, 1),
+    ("load_fz", 2, 1),
+    ("tr_gx", 1, 0, "A"),
+    ("load_gx", 1, 1),
+    ("q_fz", 0, 1),
+    ("tr_x", 0, 2, "A"),
+    ("lay_gz", 1, "V", 0, 256),
+    ("q_fx", 0, 1, 1),
+    ("q_fz", 1, 0),
+    ("q_gz", 1),
+    ("widen", 2, 3, "V"),
+    ("lay_fz", 1, 1, "A", 256, 512),
+    ("load_alpha", 0),
+    ("lay_fz", 2, 1, "A", 0, 256),
+    ("lin", 0),
+    ("q_fx", 0, 2, 2),
+    ("lin", 1),
+    ("mult", 0),
+    ("mult", 1),
+    ("tr_gx", 1, 1, "A"),
+    ("widen", 2, 1, "A"),
+    ("front", 2),
+    ("load_fx", 1, 2),
+    ("lin", 3),
+    ("lay_fz", 1, 1, "G", 0, 256),
+    ("load_rows",),
+    ("lay_fz", 2, 1, "A", 256, 512),
+    ("mult", 3),
+    ("lin", 2),
+    ("q_fz", 1, 1),
+    ("load_fx", 1, 1),
+    ("front", 7),
+    ("lin", 7),
+    ("widen", 2, 0, "V"),
+    ("tr_x", 1, 0, "A"),
+    ("lay_fz", 2, 0, "V", 0, 256),
+    ("widen", 2, 2, "A"),
+    ("mult", 2),
+    ("front", 4),
+    ("tr_c", 0, 0, "A"),
+    ("front", 5),
+    ("lin", 4),
+    ("q_gx", 1),
+    ("load_v",),
+    ("lay_gz", 2, "A", 0, 256),
+    ("tr_x", 1, 1, "V"),
+    ("mult", 7),
+    ("load_fx", 1, 3),
+    ("mult", 4),
+    ("lay_fz", 2, 0, "G", 256, 512),
+    ("tr_c", 0, 1, "A"),
+    ("q_fz", 2, 0),
+    ("q_cb", 0, 0, 2),
+    ("lay_gz", 2, "A", 256, 512),
+    ("front", 6),
+    ("tr_x", 1, 3, "A"),
+    ("lin", 5),
+    ("mult", 5),
+    ("q_fz", 2, 1),
+    ("q_gz", 2),
+    ("load_alpha", 2),
+    ("q_cb", 0, 2, 2),
+    ("lay_c", 0, "G", 256, 512),
+    ("q_fx", 1, 0, 2),
+    ("tr_x", 1, 2, "A"),
+    ("lay_c", 0, "A", 0, 256),
+    ("lin", 6),
+    ("lin", 9),
+    ("front", 9),
+    ("mult", 6),
+    ("lay_c", 1, "A", 256, 512),
+    ("front", 8),
+    ("q_fx", 1, 2, 2),
+    ("tr_c", 1, 0, "A"),
+    ("tr_c", 1, 1, "A"),
+    ("mult", 9),
+    ("lay_al", 0, "G", 0, 256),
+    ("front", 10),
+    ("front", 12),
+    ("lin", 8),
+    ("lay_al", 2, "G", 0, 256),
+    ("lin", 10),
+    ("lay_c", 1, "A", 0, 256),
+    ("mult", 8),
+    ("q_ca", 0),
+    ("mult", 10),
+    ("lay_al", 0, "G", 256, 512),
+    ("front", 11),
+    ("tr_x", "v", 3, "A"),
+    ("front", 13),
+    ("lay_al", 2, "G", 256, 512),
+    ("tr_c", 2, 0, "A"),
+    ("lin", 12),
+    ("lin", 11),
+    ("mult", 12),
+    ("load_alpha", 1),
+    ("front", 14),
+    ("lin", 13),
+    ("mult", 11),
+    ("front", 15),
+    ("lay_al", 1, "G", 256, 512),
+    ("mult", 13),
+    ("tr_x", "v", 2, "A"),
+    ("front", 17),
+    ("lay_al", 1, "A", 0, 256),
+    ("lin", 14),
+    ("mult", 14),
+    ("q_cb", 2, 0, 2),
+    ("q_cb", 1, 2, 2),
+    ("q_al", 2),
+    ("tr_c", 2, 1, "A"),
+    ("q_cb", 1, 0, 2),
+    ("lin", 15),
+    ("mult", 15),
+    ("q_al", 0),
+    ("tr_x", "v", 0, "A"),
+    ("lin", 16),
+    ("q_ca", 1),
+    ("q_al", 1),
+    ("lay_c", 2, "G", 0, 256),
+    ("q_cb", 2, 2, 2),
+    ("lay_c", 3, "G", 0, 256),
+    ("lay_c", 2, "A", 256, 512),
+    ("front", 16),
+    ("tr_x", "v", 1, "A"),
+    ("tr_c", 3, 0, "A"),
+    ("mean_mm", 0, 2),
+    ("mean_out", 0, 2, "V"),
+    ("front", 18),
+    ("mult", 16),
+    ("mean_mm", 0, 1),
+    ("mean_out", 0, 1, "A"),
+    ("lay_c", 3, "A", 256, 512),
+    ("lin", 17),
+    ("q_v",),
+    ("mult", 17),
+    ("front", 20),
+    ("front", 19),
+    ("q_cb", 3, 0, 2),
+    ("mean_mm", 0, 3),
+    ("lin", 18),
+    ("q_ca", 2),
+    ("q_ca", 3),
+    ("mean_out", 0, 3, "A"),
+    ("lin", 19),
+    ("mean_mm", 0, 0),
+    ("mult", 18),
+    ("mean_out", 0, 0, "A"),
+    ("tr_c", 3, 1, "A"),
+    ("tr_c", 4, 0, "A"),
+    ("cov_mm", 0, 3),
+    ("mult", 19),
+    ("front", 21),
+    ("lin", 20),
+    ("lin", 21),
+    ("cov_mm", 0, 0),
+    ("lay_c", 4, "A", 256, 512),
+    ("mult", 20),
+    ("lay_c", 4, "G", 0, 256),
+    ("tr_c", 4, 1, "A"),
+    ("cov_out", 0, 3, "V"),
+    ("lin", 22),
+    ("mult", 21),
+    ("cov_out", 0, 0, "A"),
+    ("q_ca", 4),
+    ("front", 22),
+    ("front", 23),
+    ("cov_mm", 1, 0),
+    ("cov_out", 1, 0, "V"),
+    ("q_cb", 3, 2, 2),
+    ("q_cb", 4, 0, 2),
+    ("lin", 23),
+    ("cov_mm", 1, 1),
+    ("cov_out", 1, 1, "A"),
+    ("tr_c", 5, 0, "A"),
+    ("mult", 22),
+    ("mult", 23),
+    ("cov_mm", 0, 1),
+    ("cov_mm", 1, 2),
+    ("mean_mm", 1, 0, (0, 1), "lin"),
+    ("cov_out", 0, 1, "V"),
+    ("cov_out", 1, 2, "V"),
+    ("cov_mm", 0, 2),
+    ("mean_mm", 1, 1, (0, 1), "lin"),
+    ("q_cb", 5, 0, 2),
+    ("cov_mm", 1, 3),
+    ("mean_mm", 1, 0, (2,)),
+    ("lay_c", 5, "A", 256, 512),
+    ("cov_out", 0, 2, "V"),
+    ("mean_mm", 1, 1, (2,)),
+    ("lay_c", 5, "A", 0, 256),
+    ("q_cb", 4, 2, 2),
+    ("cov_out", 1, 3, "V"),
+    ("q_ca", 5),
+    ("tr_c", 5, 1, "A"),
+    ("mean_out", 1, 1, "V"),
+    ("cov_mm", 2, 0),
+    ("cov_mm", 2, 2),
+    ("mean_mm", 1, 2, (0, 1), "ex"),
+    ("mean_out", 1, 0, "V"),
+    ("q_cb", 5, 2, 2),
+    ("cov_out", 2, 2, "V"),
+    ("mean_mm", 1, 2, (2,)),
+    ("cov_out", 2, 0, "A"),
+    ("mean_mm", 1, 3, (0, 1), "ex"),
+    ("mean_mm", 1, 3, (2,)),
+    ("mean_out", 1, 2, "V"),
+    ("cov_mm", 2, 1),
+    ("cov_mm", 2, 3),
+    ("mean_out", 1, 3, "V"),
+    ("cov_out", 2, 1, "V"),
+    ("cov_out", 2, 3, "V"),
+]
+
+
+def tile_gp_product_kernel_mean_f6_kernel(
+    tc, fx, fz, gx, gz_bytes, gz_scale, amp_x, amp_z, alpha, prior, scale_x, v, prec_z, out_0, out_1
+):
+    nc = tc.nc
+    G, H, S = M // B, N // B, K // B
+
+    with ExitStack() as ctx:
+        keep = ctx.enter_context(tc.tile_pool(name="keep", bufs=1))
+        work = ctx.enter_context(tc.tile_pool(name="work", bufs=2))
+        psum = ctx.enter_context(tc.psum_pool(name="psum", bufs=2))
+        ctx.enter_context(tc.manual_schedule())
+
+        def codes_and_scales(name, words):
+            codes = keep.tile([P, words], U32, name=name + "_codes", align_bytes=256)
+            scales = keep.tile([P, words], U8, name=name + "_scales", align_bytes=256)
+            return codes, scales
+
+        fx_q = codes_and_scales("fx", S * M)
+        fz_q = codes_and_scales("fz", S * N)
+        gx_q = codes_and_scales("gx", M)
+        gz_q = codes_and_scales("gz", N)
+        al_q = codes_and_scales("al", H * R)
+        v_q = codes_and_scales("v", G * Q)
+        ca_q = codes_and_scales("ca", G * N)
+        cb_q = codes_and_scales("cb", H * M)
+
+        def quantize(dst, first, in_):
+            codes, scales = dst
+            width = in_.shape[1] // 4
+            cols = slice(first, first + width)
+            nc.vector.quantize_mx(out=codes[:, cols].bitcast(FP8X4), scales=scales[:, cols], in_=in_)
+
+        def mm(out, lhs, l0, rhs, r0, start, stop):
+            nc.tensor.matmul_mx(
+                out=out,
+                lhsT=lhs[0][:, l0 : l0 + P].bitcast(FP8X4),
+                lhsT_scale=lhs[1][:, l0 : l0 + P],
+                rhs=rhs[0][:, r0 : r0 + B].bitcast(FP8X4),
+                rhs_scale=rhs[1][:, r0 : r0 + B],
+                start=start,
+                stop=stop,
+            )
+
+        warm = keep.tile([P, 1], F32, name="warm")
+        nc.gpsimd.memset(warm[:], 0.0)
+        az_rows = keep.tile([P, N], BF16, name="az_rows", align_bytes=64)
+        nc.gpsimd.memset(az_rows[:].bitcast(I32), 0)
+        ident = keep.tile([P, P], F32, name="ident")
+        make_identity(nc, ident[:])
+        ones = keep.tile([P, P], BF16, name="ones")
+        nc.gpsimd.memset(ones[:], 1.0)
+        warm2 = keep.tile([P, 1], F32, name="warm2")
+        nc.scalar.activation(out=warm2[:], in_=warm[:], func=ACT.Exp)
+
+        gzs = keep.tile([P, 4], F32, name="gzs")
+        nc.scalar.dma_start(out=gzs[:], in_=gz_scale.rearrange("(p j) o -> p (j o)", j=4))
+        ax16 = keep.tile([P, G, 4], BF16, name="ax16")
+        nc.scalar.dma_start(out=ax16[:], in_=amp_x.rearrange("(g p t) -> p g t", p=P, t=4))
+        sx16 = keep.tile([P, G, 4], BF16, name="sx16")
+        nc.scalar.dma_start(out=sx16[:], in_=scale_x.rearrange("(g p t) -> p g t", p=P, t=4))
+        nc.scalar.dma_start(out=az_rows[0:1, :], in_=amp_z.rearrange("(o n) -> o n", o=1))
+
+        gz_v = gz_bytes.rearrange("(p j) n -> p j n", j=4)
+        fz_v = fz.rearrange("(s p j) n -> s p j n", p=P, j=4)
+        fx_v = fx.rearrange("(g p t) k -> g p t k", p=P, t=4)
+        gx_v = gx.rearrange("(g p t) d -> g p t d", p=P, t=4)
+        al_v = alpha.rearrange("(h p j) r -> h p j r", p=P, j=4)
+        v_v = v.rearrange("(p b) m -> p b m", b=4)
+        gxr, fzr, xr, alr = {}, {}, {}, {}
+
+        def tile_for(store, key, shape, dtype, tag, bufs):
+            if key not in store:
+                store[key] = work.tile(shape, dtype, name=tag, tag=tag, bufs=bufs, align_bytes=64)
+            return store[key]
+
+        def load_gx(g, pair):
+            tile_for(gxr, g, [P, 4, D], BF16, "gxr", 2)
+            t = slice(2 * pair, 2 * pair + 2)
+            nc.sync.dma_start(out=gxr[g][:, t], in_=gx_v[g][:, t])
+
+        def load_fz(h, s):
+            tile_for(fzr, h, [P, S, 4, B], BF16, "fzr", 3)
+            nc.sync.dma_start(out=fzr[h][:, s], in_=fz_v[s][:, :, h * B : (h + 1) * B])
+
+        def load_fx(g, t):
+            tile_for(xr, g, [P, 4, K], BF16, "xr", 2)
+            nc.sync.dma_start(out=xr[g][:, t], in_=fx_v[g][:, t])
+
+        gzb = {}
+
+        def load_gz(h):
+            gzb[h] = keep.tile([P, 4, B], U8, name="gzb%d" % h)
+            nc.sync.dma_start(out=gzb[h][:], in_=gz_v[:, :, h * B : (h + 1) * B])
+
+        def load_alpha(h):
+            alr[h] = work.tile([P, 4, R], BF16, name="alr", tag="alr", bufs=3, align_bytes=64)
+            nc.sync.dma_start(out=alr[h][:], in_=al_v[h])
+
+        prec_b = keep.tile([P, N], BF16, name="prec_b", align_bytes=64)
+        prior_b = keep.tile([P, R], BF16, name="prior_b", align_bytes=64)
+
+        def load_v():
+            xr["v"] = work.tile([P, 4, M], BF16, name="xr", tag="xr", bufs=2, align_bytes=64)
+            nc.sync.dma_start(out=xr["v"][:], in_=v_v)
+
+        def load_rows():
+            nc.sync.dma_start(out=prior_b[:], in_=prior.partition_broadcast(P))
+            nc.sync.dma_start(out=prec_b[:], in_=prec_z.partition_broadcast(P))
+
+        ax = keep.tile([P, G, 4], F32, name="ax")
+        nc.gpsimd.tensor_copy(out=ax[:], in_=ax16[:])
+        sx = keep.tile([P, G, 4], F32, name="sx")
+        nc.gpsimd.tensor_copy(out=sx[:], in_=sx16[:])
+        az_b = keep.tile([P, N], BF16, name="az_b", align_bytes=64)
+
+        def copy_on(eng, out, in_):
+            if eng == "A":
+                nc.scalar.copy(out=out, in_=in_)
+            elif eng == "V":
+                nc.vector.tensor_copy(out=out, in_=in_)
+            else:
+                nc.gpsimd.tensor_scalar(out=out, in0=in_, scalar1=1.0, scalar2=0.0, op0=ALU.mult, op1=ALU.add)
+
+        def spread_az(h):
+            bank = psum.tile([P, B], F32, name="acc", tag="acc", bufs=2)
+            nc.tensor.matmul(out=bank[:], lhsT=ones[:], rhs=az_rows[:, h * B : (h + 1) * B], start=True, stop=True)
+            nc.scalar.copy(out=az_b[:, h * B : (h + 1) * B], in_=bank[:])
+
+        def turn(words, firsts, grouped, eng="A"):
+            bank = psum.tile([P, 4, P], F32, name="tr", tag="tr", bufs=2)
+            for i in range(4):
+                nc.tensor.transpose(bank[:, i, :], words[i // 2][:, firsts[i // 2] + i % 2 : firsts[i // 2] + 256 : 2], ident[:])
+            out = grouped.rearrange("p a m j -> p a (m j)").bitcast(F32).rearrange("p a (m u) -> p a m u", u=2)
+            copy_on(eng, out, bank[:].rearrange("p (a u) m -> p a m u", u=2))
+
+        gxg, xg, mix, gzw = {}, {}, {}, {}
+
+        def tr_gx(g, pair, eng="A"):
+            tile_for(gxg, g, [P, 4, P, 4], BF16, "mix", 4)
+            words = [gxr[g][:, 2 * pair + i, :].bitcast(F32) for i in range(2)]
+            turn(words, (0, 0), gxg[g][:, 2 * pair : 2 * pair + 2], eng)
+
+        def q_gx(g):
+            quantize(gx_q, g * B, gxg[g][:].rearrange("p t m j -> p (t m j)"))
+
+        def tr_x(g, t, eng="A"):
+            tile_for(xg, g, [P, 4, S, P, 4], BF16, "xg", 1)
+            words = xr[g][:, t, :].bitcast(F32)
+            turn([words, words], (0, 256), xg[g][:, t], eng)
+
+        def q_fx(g, t0, n):
+            quantize(fx_q, (g * 4 + t0) * S * P, xg[g][:, t0 : t0 + n].rearrange("p t s m j -> p (t s m j)"))
+
+        def q_v():
+            quantize(v_q, 0, xg["v"][:].rearrange("p t s m j -> p (t s m j)"))
+
+        def mixed(key):
+            if key not in mix:
+                mix[key] = work.tile([P, B, 4], BF16, name="mix", tag="mix", bufs=4, align_bytes=64)
+            return mix[key]
+
+        def lay(key, src, eng, a=0, b=B):
+            copy_on(eng, mixed(key)[:, a:b, :], src[:, :, a:b].rearrange("p j n -> p n j"))
+
+        def q_lay(dst, first, key):
+            quantize(dst, first, mix[key][:].rearrange("p n j -> p (n j)"))
+
+        def widen(h, j, eng="A"):
+            tile_for(gzw, h, [P, 4, B], BF16, "gzw", 2)
+            src = gzb[h][:, j, :].bitcast(FP8)
+            if eng == "V":
+                nc.vector.tensor_scalar(out=gzw[h][:, j, :], in0=src, scalar1=gzs[:, j : j + 1], scalar2=None, op0=ALU.mult)
+            else:
+                nc.scalar.activation(out=gzw[h][:, j, :], in_=src, func=ACT.Copy, scale=gzs[:, j : j + 1])
+
+        def lay_gz(h, eng, a=0, b=B):
+            lay(("gz", h), gzw[h], eng, a, b)
+
+        def q_gz(h):
+            q_lay(gz_q, h * B, ("gz", h))
+
+        def lay_fz(h, s, eng, a=0, b=B):
+            lay(("fz", h, s), fzr[h][:, s], eng, a, b)
+
+        def q_fz(h, s):
+            q_lay(fz_q, (h * S + s) * B, ("fz", h, s))
+
+        def lay_al(h, eng, a=0, b=B):
+            lay(("al", h), alr[h], eng, a, b)
+
+        def q_al(h):
+            q_lay(al_q, h * R, ("al", h))
+
+        ex_b, lin_b, x_t, e_t, c_nat, cag, cbg = {}, {}, {}, {}, {}, {}, {}
+
+        def where(i):
+            k, t = i // 4, i % 4
+            return k // H, k % H, t
+
+        def front(i):
+            g, h, t = where(i)
+            ex_b[i] = psum.tile([P, B], F32, name="ex", tag="ex", bufs=2)
+            mm(ex_b[i][:], gx_q, (g * 4 + t) * P, gz_q, h * B, True, True)
+            add(i)
+            exp(i)
+
+        def lin(i):
+            g, h, t = where(i)
+            lin_b[i] = psum.tile([P, B], F32, name="lin", tag="lin", bufs=2)
+            for s in range(S):
+                mm(lin_b[i][:], fx_q, ((g * 4 + t) * S + s) * P, fz_q, (h * S + s) * B, s == 0, s == S - 1)
+
+        def add(i):
+            g, h, t = where(i)
+            x_t[i] = work.tile([P, B], F32, name="xt", tag="xt", bufs=2)
+            nc.vector.tensor_tensor(out=x_t[i][:], in0=ex_b[i][:], in1=az_b[:, h * B : (h + 1) * B], op=ALU.add)
+
+        def exp(i):
+            g, h, t = where(i)
+            e_t[i] = work.tile([P, B], F32, name="et", tag="et", bufs=3)
+            nc.scalar.activation(out=e_t[i][:], in_=x_t[i][:], func=ACT.Exp, bias=ax[:, g, t : t + 1])
+
+        def mult(i):
+            k, t = i // 4, i % 4
+            tile_for(c_nat, k, [P, 4, B], BF16, "cnat", 2)
+            nc.vector.tensor_tensor(out=c_nat[k][:, t, :], in0=lin_b[i][:], in1=e_t[i][:], op=ALU.mult)
+
+        def tr_c(k, pair, eng="A"):
+            tile_for(cbg, k, [P, 4, P, 4], BF16, "cbg", 2)
+            words = [c_nat[k][:, 2 * pair + i, :].bitcast(F32) for i in range(2)]
+            turn(words, (0, 0), cbg[k][:, 2 * pair : 2 * pair + 2], eng)
+
+        def lay_c(k, eng, a=0, b=B):
+            if k not in cag:
+                cag[k] = work.tile([P, B, 4], BF16, name="cag", tag="cag", bufs=2, align_bytes=64)
+            copy_on(eng, cag[k][:, a:b, :], c_nat[k][:, :, a:b].rearrange("p t n -> p n t"))
+
+        def q_ca(k):
+            quantize(ca_q, k * B, cag[k][:].rearrange("p n t -> p (n t)"))
+
+        def q_cb(k, t0=0, n=4):
+            g, h = k // H, k % H
+            quantize(cb_q, (h * G + g) * B + t0 * P, cbg[k][:, t0 : t0 + n].rearrange("p t m j -> p (t m j)"))
+
+        acc = {}
+        cov_v = out_1.rearrange("(p b) n -> b p n", b=4)
+        mean_v = out_0.rearrange("(g p t) r -> g t p r", p=P, t=4)
+
+        def cov_mm(h, b, tag="acc"):
+            acc["cov", h, b] = psum.tile([P, B], F32, name=tag, tag=tag, bufs=2)
+            for g in range(G):
+                mm(acc["cov", h, b][:], v_q, (b * G + g) * P, ca_q, (g * H + h) * B, g == 0, g == G - 1)
+
+        res = {}
+
+        def result(key, i):
+            return tile_for(res, key, [P, 4, B], F32, "fzr", 3)[:, i, :]
+
+        def cov_out(h, b, eng="V"):
+            o = result(("cov", h), b)
+            if eng == "V":
+                nc.vector.tensor_tensor(out=o, in0=acc["cov", h, b][:], in1=prec_b[:, h * B : (h + 1) * B], op=ALU.mult)
+            else:
+                m = work.tile([P, B], F32, name="mid", tag="mid", bufs=2)
+                nc.scalar.copy(out=m[:], in_=acc["cov", h, b][:])
+                nc.gpsimd.tensor_tensor(out=o, in0=m[:], in1=prec_b[:, h * B : (h + 1) * B], op=ALU.mult)
+            nc.sync.dma_start(out=cov_v[b][:, h * B : (h + 1) * B], in_=o)
+
+        def mean_mm(g, t, hs=(0, 1, 2), tag="acc"):
+            if hs[0] == 0:
+                acc["mean", g, t] = psum.tile([P, R], F32, name=tag, tag=tag, bufs=2)
+            for h in hs:
+                mm(acc["mean", g, t][:], cb_q, (h * G + g) * B + t * P, al_q, h * R, h == 0, h == H - 1)
+
+        def mean_out(g, t, eng="V"):
+            o = result(("mean", g), t)
+            if eng == "V":
+                nc.vector.scalar_tensor_tensor(
+                    out=o, in0=acc["mean", g, t][:], scalar=sx[:, g, t : t + 1], in1=prior_b[:], op0=ALU.mult, op1=ALU.add
+                )
+            else:
+                m = work.tile([P, B], F32, name="mid", tag="mid", bufs=2)
+                nc.scalar.activation(out=m[:], in_=acc["mean", g, t][:], func=ACT.Copy, scale=sx[:, g, t : t + 1])
+                nc.gpsimd.tensor_tensor(out=o, in0=m[:], in1=prior_b[:], op=ALU.add)
+            nc.sync.dma_start(out=mean_v[g, t], in_=o)
+
+        ops = dict(
+            widen=widen, tr_gx=tr_gx, tr_x=tr_x, lay_gz=lay_gz, lay_fz=lay_fz, lay_al=lay_al, lay_c=lay_c, q_gx=q_gx, q_fx=q_fx,
+            q_v=q_v, q_gz=q_gz, q_fz=q_fz, q_al=q_al, q_ca=q_ca, q_cb=q_cb, spread_az=spread_az, front=front, lin=lin, mult=mult,
+            tr_c=tr_c, cov_mm=cov_mm, cov_out=cov_out, mean_mm=mean_mm, mean_out=mean_out, load_gx=load_gx, load_fz=load_fz, load_fx=load_fx, load_gz=load_gz,
+            load_alpha=load_alpha, load_v=load_v, load_rows=load_rows,
+        )
+        for name, *args in SEQ:
+            ops[name](*args)

@@ -21,264 +21,264 @@ B = 512
 
 
 SEQ = [
-    ("spread_az", 0),
-    ("load_gz", 1),
-    ("spread_az", 1),
     ("load_gz", 0),
-    ("load_gx", 0, 0),
-    ("load_fz", 0, 0),
-    ("widen", 1, 1, "V"),
-    ("widen", 1, 2, "V"),
-    ("load_gx", 0, 1),
-    ("widen", 0, 1, "V"),
-    ("widen", 0, 3, "A"),
-    ("widen", 0, 0, "V"),
     ("widen", 0, 2, "V"),
-    ("load_fz", 0, 1),
-    ("spread_az", 2),
-    ("widen", 1, 0, "V"),
-    ("load_fx", 0, 0),
-    ("lay_gz", 0, "V", 256, 512),
+    ("load_gx", 0, 1),
+    ("widen", 0, 3, "V"),
+    ("load_fz", 0, 0),
+    ("load_gx", 0, 0),
+    ("widen", 0, 1, "V"),
+    ("widen", 0, 0, "A"),
     ("load_fx", 0, 1),
-    ("lay_fz", 0, 0, "V", 0, 256),
-    ("tr_gx", 0, 0, "V"),
-    ("load_fz", 1, 0),
-    ("lay_gz", 0, "A", 0, 256),
-    ("q_gz", 0),
-    ("lay_fz", 0, 0, "V", 256, 512),
+    ("spread_az", 1),
+    ("spread_az", 0),
     ("tr_gx", 0, 1, "A"),
-    ("q_gx", 0),
-    ("q_fz", 0, 0),
-    ("lay_fz", 0, 1, "A", 0, 256),
-    ("tr_x", 0, 0, "A"),
-    ("lay_fz", 0, 1, "A", 256, 512),
-    ("front", 0),
-    ("load_gx", 1, 0),
-    ("widen", 1, 3, "A"),
-    ("lay_fz", 1, 0, "G", 0, 256),
-    ("lay_fz", 1, 0, "G", 256, 512),
-    ("tr_x", 0, 1, "V"),
-    ("front", 1),
-    ("load_fx", 1, 0),
-    ("lay_gz", 1, "A", 256, 512),
-    ("load_fx", 0, 3),
-    ("load_fz", 2, 0),
+    ("load_gz", 1),
+    ("spread_az", 2),
+    ("lay_gz", 0, "V", 0, 256),
+    ("tr_gx", 0, 0, "A"),
     ("load_fx", 0, 2),
+    ("lay_gz", 0, "V", 256, 512),
+    ("widen", 1, 1, "A"),
+    ("load_fx", 0, 0),
+    ("tr_x", 0, 1, "A"),
+    ("lay_fz", 0, 0, "V", 0, 256),
+    ("lay_fz", 0, 0, "V", 256, 512),
+    ("widen", 1, 2, "A"),
+    ("tr_x", 0, 0, "A"),
+    ("q_gz", 0),
+    ("load_fx", 0, 3),
+    ("load_gz", 2),
+    ("widen", 1, 0, "V"),
+    ("q_gx", 0),
+    ("q_fx", 0, 1, 1),
+    ("widen", 2, 1, "A"),
+    ("widen", 1, 3, "V"),
+    ("tr_x", 0, 3, "A"),
+    ("widen", 2, 0, "V"),
+    ("load_fz", 0, 1),
+    ("front", 1),
+    ("load_fx", 1, 1),
+    ("lay_fz", 0, 1, "A", 0, 256),
+    ("lay_fz", 0, 1, "V", 256, 512),
+    ("load_gx", 1, 1),
+    ("front", 0),
+    ("lay_gz", 1, "A", 256, 512),
+    ("tr_x", 0, 2, "A"),
     ("front", 3),
     ("load_fz", 1, 1),
-    ("load_gz", 2),
-    ("tr_x", 0, 3, "V"),
+    ("load_fz", 1, 0),
     ("q_fx", 0, 0, 1),
-    ("load_fz", 2, 1),
-    ("tr_gx", 1, 0, "A"),
-    ("load_gx", 1, 1),
+    ("load_v",),
     ("q_fz", 0, 1),
-    ("tr_x", 0, 2, "A"),
-    ("lay_gz", 1, "V", 0, 256),
-    ("q_fx", 0, 1, 1),
-    ("q_fz", 1, 0),
-    ("q_gz", 1),
-    ("widen", 2, 3, "V"),
-    ("lay_fz", 1, 1, "A", 256, 512),
-    ("load_alpha", 0),
-    ("lay_fz", 2, 1, "A", 0, 256),
-    ("lin", 0),
-    ("q_fx", 0, 2, 2),
+    ("load_fz", 2, 0),
+    ("load_gx", 1, 0),
+    ("q_fz", 0, 0),
     ("lin", 1),
-    ("mult", 0),
-    ("mult", 1),
-    ("tr_gx", 1, 1, "A"),
-    ("widen", 2, 1, "A"),
-    ("front", 2),
-    ("load_fx", 1, 2),
-    ("lin", 3),
-    ("lay_fz", 1, 1, "G", 0, 256),
-    ("load_rows",),
-    ("lay_fz", 2, 1, "A", 256, 512),
-    ("mult", 3),
-    ("lin", 2),
-    ("q_fz", 1, 1),
-    ("load_fx", 1, 1),
-    ("front", 7),
-    ("lin", 7),
-    ("widen", 2, 0, "V"),
-    ("tr_x", 1, 0, "A"),
-    ("lay_fz", 2, 0, "V", 0, 256),
+    ("lay_fz", 1, 0, "V", 0, 256),
     ("widen", 2, 2, "A"),
+    ("lay_fz", 1, 1, "V", 0, 256),
+    ("q_fx", 0, 2, 2),
+    ("lay_fz", 1, 0, "A", 256, 512),
+    ("lay_gz", 1, "V", 0, 256),
+    ("lin", 0),
+    ("mult", 1),
+    ("tr_x", 1, 1, "A"),
+    ("front", 2),
+    ("lay_fz", 1, 1, "V", 256, 512),
+    ("lay_fz", 2, 0, "A", 0, 256),
+    ("mult", 0),
+    ("q_fz", 1, 0),
+    ("widen", 2, 3, "A"),
+    ("load_alpha", 0),
+    ("lin", 3),
+    ("load_alpha", 1),
+    ("load_fx", 1, 0),
+    ("q_gz", 1),
+    ("q_fz", 1, 1),
+    ("load_fz", 2, 1),
+    ("mult", 3),
+    ("lay_fz", 2, 0, "V", 256, 512),
+    ("tr_gx", 1, 1, "A"),
+    ("lay_gz", 2, "A", 256, 512),
+    ("lay_fz", 2, 1, "A", 256, 512),
+    ("front", 5),
+    ("q_fz", 2, 0),
+    ("tr_x", 1, 0, "A"),
+    ("lay_gz", 2, "V", 0, 256),
+    ("lay_fz", 2, 1, "V", 0, 256),
+    ("lin", 5),
+    ("lay_al", 1, "A", 256, 512),
+    ("lin", 2),
+    ("tr_gx", 1, 0, "A"),
+    ("mult", 5),
     ("mult", 2),
     ("front", 4),
-    ("tr_c", 0, 0, "A"),
-    ("front", 5),
-    ("lin", 4),
-    ("q_gx", 1),
-    ("load_v",),
-    ("lay_gz", 2, "A", 0, 256),
-    ("tr_x", 1, 1, "V"),
-    ("mult", 7),
-    ("load_fx", 1, 3),
-    ("mult", 4),
-    ("lay_fz", 2, 0, "G", 256, 512),
-    ("tr_c", 0, 1, "A"),
-    ("q_fz", 2, 0),
-    ("q_cb", 0, 0, 2),
-    ("lay_gz", 2, "A", 256, 512),
-    ("front", 6),
-    ("tr_x", 1, 3, "A"),
-    ("lin", 5),
-    ("mult", 5),
-    ("q_fz", 2, 1),
+    ("lay_c", 0, "A", 256, 512),
     ("q_gz", 2),
+    ("lin", 4),
+    ("q_fz", 2, 1),
     ("load_alpha", 2),
-    ("q_cb", 0, 2, 2),
-    ("lay_c", 0, "G", 256, 512),
-    ("q_fx", 1, 0, 2),
-    ("tr_x", 1, 2, "A"),
-    ("lay_c", 0, "A", 0, 256),
+    ("load_fx", 1, 3),
+    ("front", 7),
+    ("lin", 7),
+    ("mult", 4),
+    ("tr_c", 0, 1, "A"),
+    ("front", 6),
+    ("mult", 7),
+    ("tr_c", 0, 0, "A"),
+    ("front", 9),
     ("lin", 6),
     ("lin", 9),
-    ("front", 9),
-    ("mult", 6),
-    ("lay_c", 1, "A", 256, 512),
-    ("front", 8),
-    ("q_fx", 1, 2, 2),
-    ("tr_c", 1, 0, "A"),
-    ("tr_c", 1, 1, "A"),
-    ("mult", 9),
-    ("lay_al", 0, "G", 0, 256),
-    ("front", 10),
-    ("front", 12),
-    ("lin", 8),
-    ("lay_al", 2, "G", 0, 256),
-    ("lin", 10),
-    ("lay_c", 1, "A", 0, 256),
-    ("mult", 8),
-    ("q_ca", 0),
-    ("mult", 10),
-    ("lay_al", 0, "G", 256, 512),
-    ("front", 11),
-    ("tr_x", "v", 3, "A"),
-    ("front", 13),
-    ("lay_al", 2, "G", 256, 512),
-    ("tr_c", 2, 0, "A"),
-    ("lin", 12),
-    ("lin", 11),
-    ("mult", 12),
-    ("load_alpha", 1),
-    ("front", 14),
-    ("lin", 13),
-    ("mult", 11),
-    ("front", 15),
-    ("lay_al", 1, "G", 256, 512),
-    ("mult", 13),
-    ("tr_x", "v", 2, "A"),
-    ("front", 17),
+    ("q_gx", 1),
+    ("load_fx", 1, 2),
     ("lay_al", 1, "A", 0, 256),
-    ("lin", 14),
-    ("mult", 14),
-    ("q_cb", 2, 0, 2),
-    ("q_cb", 1, 2, 2),
-    ("q_al", 2),
-    ("tr_c", 2, 1, "A"),
-    ("q_cb", 1, 0, 2),
-    ("lin", 15),
-    ("mult", 15),
-    ("q_al", 0),
-    ("tr_x", "v", 0, "A"),
-    ("lin", 16),
+    ("tr_c", 1, 0, "A"),
+    ("mult", 6),
+    ("lay_c", 0, "V", 0, 256),
+    ("tr_x", 1, 2, "A"),
+    ("front", 8),
+    ("lay_c", 1, "V", 256, 512),
+    ("front", 11),
+    ("lin", 11),
+    ("q_cb", 0, 0, 2),
+    ("mult", 9),
+    ("tr_c", 1, 1, "A"),
+    ("lay_al", 0, "A", 0, 256),
+    ("q_cb", 0, 2, 2),
+    ("tr_x", 1, 3, "A"),
+    ("front", 10),
+    ("lay_al", 2, "A", 256, 512),
+    ("q_fx", 1, 0, 2),
+    ("lin", 8),
+    ("lay_al", 2, "V", 0, 256),
+    ("mult", 11),
+    ("lay_c", 1, "A", 0, 256),
+    ("q_fx", 1, 2, 2),
+    ("mult", 8),
+    ("lin", 12),
+    ("front", 12),
+    ("front", 13),
+    ("lin", 10),
+    ("tr_x", "v", 3, "A"),
+    ("mult", 10),
     ("q_ca", 1),
+    ("front", 15),
+    ("mult", 12),
+    ("tr_c", 2, 1, "A"),
+    ("lay_al", 0, "A", 256, 512),
+    ("q_ca", 0),
+    ("front", 14),
+    ("tr_c", 2, 0, "A"),
+    ("lin", 13),
+    ("q_al", 2),
     ("q_al", 1),
-    ("lay_c", 2, "G", 0, 256),
-    ("q_cb", 2, 2, 2),
-    ("lay_c", 3, "G", 0, 256),
+    ("mult", 13),
+    ("tr_x", "v", 0, "A"),
+    ("lay_c", 2, "A", 0, 256),
+    ("q_al", 0),
+    ("front", 17),
+    ("load_rows",),
+    ("lin", 14),
+    ("q_cb", 2, 0, 2),
+    ("lin", 15),
+    ("mult", 14),
     ("lay_c", 2, "A", 256, 512),
+    ("tr_x", "v", 2, "A"),
+    ("mult", 15),
     ("front", 16),
-    ("tr_x", "v", 1, "A"),
-    ("tr_c", 3, 0, "A"),
-    ("mean_mm", 0, 2),
-    ("mean_out", 0, 2, "V"),
-    ("front", 18),
-    ("mult", 16),
-    ("mean_mm", 0, 1),
-    ("mean_out", 0, 1, "A"),
-    ("lay_c", 3, "A", 256, 512),
-    ("lin", 17),
-    ("q_v",),
-    ("mult", 17),
-    ("front", 20),
+    ("q_cb", 1, 0, 2),
     ("front", 19),
-    ("q_cb", 3, 0, 2),
-    ("mean_mm", 0, 3),
-    ("lin", 18),
-    ("q_ca", 2),
-    ("q_ca", 3),
-    ("mean_out", 0, 3, "A"),
+    ("lay_c", 3, "A", 256, 512),
+    ("lay_c", 3, "A", 0, 256),
+    ("lin", 17),
+    ("tr_x", "v", 1, "A"),
+    ("mean_mm", 0, 1),
+    ("q_cb", 1, 2, 2),
+    ("lin", 16),
+    ("q_cb", 2, 2, 2),
+    ("mult", 17),
+    ("mean_out", 0, 1, "V"),
     ("lin", 19),
-    ("mean_mm", 0, 0),
-    ("mult", 18),
-    ("mean_out", 0, 0, "A"),
-    ("tr_c", 3, 1, "A"),
-    ("tr_c", 4, 0, "A"),
-    ("cov_mm", 0, 3),
+    ("mult", 16),
+    ("front", 20),
+    ("mean_mm", 0, 2),
     ("mult", 19),
-    ("front", 21),
+    ("front", 18),
+    ("mean_mm", 0, 0),
+    ("q_ca", 2),
+    ("tr_c", 3, 0, "A"),
+    ("lin", 18),
+    ("mean_out", 0, 0, "V"),
+    ("mean_out", 0, 2, "V"),
+    ("q_ca", 3),
     ("lin", 20),
-    ("lin", 21),
-    ("cov_mm", 0, 0),
+    ("mult", 18),
+    ("tr_c", 3, 1, "A"),
     ("lay_c", 4, "A", 256, 512),
     ("mult", 20),
-    ("lay_c", 4, "G", 0, 256),
+    ("q_v",),
     ("tr_c", 4, 1, "A"),
-    ("cov_out", 0, 3, "V"),
-    ("lin", 22),
-    ("mult", 21),
-    ("cov_out", 0, 0, "A"),
-    ("q_ca", 4),
-    ("front", 22),
-    ("front", 23),
-    ("cov_mm", 1, 0),
-    ("cov_out", 1, 0, "V"),
+    ("mean_mm", 0, 3),
+    ("tr_c", 4, 0, "A"),
+    ("q_cb", 3, 0, 2),
+    ("lay_c", 4, "A", 0, 256),
+    ("mean_out", 0, 3, "V"),
     ("q_cb", 3, 2, 2),
+    ("front", 23),
+    ("front", 21),
+    ("cov_mm", 0, 0),
+    ("cov_out", 0, 0, "V"),
     ("q_cb", 4, 0, 2),
-    ("lin", 23),
+    ("q_ca", 4),
+    ("cov_mm", 0, 3),
+    ("lin", 21),
+    ("mult", 21),
+    ("front", 22),
+    ("lin", 22),
     ("cov_mm", 1, 1),
-    ("cov_out", 1, 1, "A"),
     ("tr_c", 5, 0, "A"),
-    ("mult", 22),
-    ("mult", 23),
-    ("cov_mm", 0, 1),
+    ("cov_out", 0, 3, "V"),
+    ("lin", 23),
+    ("cov_out", 1, 1, "V"),
     ("cov_mm", 1, 2),
-    ("mean_mm", 1, 0, (0, 1), "lin"),
-    ("cov_out", 0, 1, "V"),
+    ("mult", 22),
     ("cov_out", 1, 2, "V"),
-    ("cov_mm", 0, 2),
-    ("mean_mm", 1, 1, (0, 1), "lin"),
-    ("q_cb", 5, 0, 2),
-    ("cov_mm", 1, 3),
-    ("mean_mm", 1, 0, (2,)),
+    ("cov_mm", 1, 0),
+    ("mult", 23),
+    ("mean_mm", 1, 0, (0, 1), "lin"),
+    ("cov_out", 1, 0, "V"),
+    ("cov_mm", 0, 1),
     ("lay_c", 5, "A", 256, 512),
+    ("q_cb", 5, 0, 2),
+    ("cov_mm", 0, 2),
+    ("mean_mm", 1, 0, (2,)),
+    ("cov_out", 0, 1, "V"),
     ("cov_out", 0, 2, "V"),
-    ("mean_mm", 1, 1, (2,)),
     ("lay_c", 5, "A", 0, 256),
+    ("mean_mm", 1, 1, (0, 1), "lin"),
     ("q_cb", 4, 2, 2),
-    ("cov_out", 1, 3, "V"),
-    ("q_ca", 5),
+    ("cov_mm", 1, 3),
     ("tr_c", 5, 1, "A"),
-    ("mean_out", 1, 1, "V"),
-    ("cov_mm", 2, 0),
-    ("cov_mm", 2, 2),
-    ("mean_mm", 1, 2, (0, 1), "ex"),
     ("mean_out", 1, 0, "V"),
+    ("q_ca", 5),
+    ("cov_out", 1, 3, "V"),
     ("q_cb", 5, 2, 2),
-    ("cov_out", 2, 2, "V"),
-    ("mean_mm", 1, 2, (2,)),
-    ("cov_out", 2, 0, "A"),
+    ("mean_mm", 1, 1, (2,)),
     ("mean_mm", 1, 3, (0, 1), "ex"),
-    ("mean_mm", 1, 3, (2,)),
-    ("mean_out", 1, 2, "V"),
+    ("cov_mm", 2, 2),
+    ("mean_out", 1, 1, "V"),
     ("cov_mm", 2, 1),
-    ("cov_mm", 2, 3),
-    ("mean_out", 1, 3, "V"),
+    ("cov_out", 2, 2, "V"),
+    ("mean_mm", 1, 3, (2,)),
+    ("mean_mm", 1, 2, (0, 1), "ex"),
     ("cov_out", 2, 1, "V"),
+    ("mean_out", 1, 3, "V"),
+    ("cov_mm", 2, 0),
+    ("mean_mm", 1, 2, (2,)),
+    ("cov_out", 2, 0, "V"),
+    ("mean_out", 1, 2, "V"),
+    ("cov_mm", 2, 3),
     ("cov_out", 2, 3, "V"),
 ]
 

@@ -22,264 +22,254 @@ B = 512
 
 SEQ = [
     ("load_gz", 0),
-    ("widen", 0, 2, "V"),
-    ("load_gx", 0, 1),
-    ("widen", 0, 3, "V"),
     ("load_fz", 0, 0),
-    ("load_gx", 0, 0),
     ("widen", 0, 1, "V"),
-    ("widen", 0, 0, "A"),
-    ("load_fx", 0, 1),
-    ("spread_az", 1),
-    ("spread_az", 0),
-    ("tr_gx", 0, 1, "A"),
-    ("load_gz", 1),
-    ("spread_az", 2),
-    ("lay_gz", 0, "V", 0, 256),
-    ("tr_gx", 0, 0, "A"),
-    ("load_fx", 0, 2),
-    ("lay_gz", 0, "V", 256, 512),
-    ("widen", 1, 1, "A"),
-    ("load_fx", 0, 0),
-    ("tr_x", 0, 1, "A"),
-    ("lay_fz", 0, 0, "V", 0, 256),
+    ("widen", 0, 2, "V"),
+    ("widen", 0, 0, "V"),
+    ("load_fx", 0, 0, 2),
     ("lay_fz", 0, 0, "V", 256, 512),
-    ("widen", 1, 2, "A"),
+    ("load_gx", 0),
+    ("widen", 0, 3, "V"),
+    ("lay_fz", 0, 0, "V", 0, 256),
+    ("spread_az", 0),
+    ("load_fz", 0, 1),
+    ("lay_gz", 0, "A", 0, 256),
+    ("q_fz", 0, 0),
     ("tr_x", 0, 0, "A"),
+    ("lay_gz", 0, "V", 256, 512),
+    ("load_fx", 0, 2, 2),
+    ("tr_x", 0, 1, "A"),
+    ("spread_az", 1),
     ("q_gz", 0),
-    ("load_fx", 0, 3),
-    ("load_gz", 2),
-    ("widen", 1, 0, "V"),
+    ("load_gz", 1),
+    ("load_fz", 1, 1),
+    ("tr_gx", 0, 0, "A"),
+    ("load_fz", 1, 0),
+    ("lay_fz", 0, 1, "V", 0, 256),
+    ("lay_fz", 0, 1, "V", 256, 512),
+    ("q_fx", 0, 0, 1),
+    ("tr_gx", 0, 1, "A"),
+    ("tr_x", 0, 3, "A"),
+    ("tr_x", 0, 2, "A"),
+    ("widen", 1, 1, "A"),
+    ("lay_fz", 1, 1, "G", 256, 512),
+    ("widen", 1, 0, "A"),
+    ("load_fx", 1, 0, 4),
+    ("q_fz", 0, 1),
     ("q_gx", 0),
     ("q_fx", 0, 1, 1),
-    ("widen", 2, 1, "A"),
-    ("widen", 1, 3, "V"),
-    ("tr_x", 0, 3, "A"),
-    ("widen", 2, 0, "V"),
-    ("load_fz", 0, 1),
-    ("front", 1),
-    ("load_fx", 1, 1),
-    ("lay_fz", 0, 1, "A", 0, 256),
-    ("lay_fz", 0, 1, "V", 256, 512),
-    ("load_gx", 1, 1),
-    ("front", 0),
-    ("lay_gz", 1, "A", 256, 512),
-    ("tr_x", 0, 2, "A"),
-    ("front", 3),
-    ("load_fz", 1, 1),
-    ("load_fz", 1, 0),
-    ("q_fx", 0, 0, 1),
-    ("load_v",),
-    ("q_fz", 0, 1),
-    ("load_fz", 2, 0),
-    ("load_gx", 1, 0),
-    ("q_fz", 0, 0),
-    ("lin", 1),
-    ("lay_fz", 1, 0, "V", 0, 256),
-    ("widen", 2, 2, "A"),
-    ("lay_fz", 1, 1, "V", 0, 256),
-    ("q_fx", 0, 2, 2),
-    ("lay_fz", 1, 0, "A", 256, 512),
-    ("lay_gz", 1, "V", 0, 256),
-    ("lin", 0),
-    ("mult", 1),
-    ("tr_x", 1, 1, "A"),
-    ("front", 2),
-    ("lay_fz", 1, 1, "V", 256, 512),
-    ("lay_fz", 2, 0, "A", 0, 256),
-    ("mult", 0),
-    ("q_fz", 1, 0),
-    ("widen", 2, 3, "A"),
-    ("load_alpha", 0),
-    ("lin", 3),
     ("load_alpha", 1),
-    ("load_fx", 1, 0),
-    ("q_gz", 1),
-    ("q_fz", 1, 1),
-    ("load_fz", 2, 1),
-    ("mult", 3),
-    ("lay_fz", 2, 0, "V", 256, 512),
-    ("tr_gx", 1, 1, "A"),
-    ("lay_gz", 2, "A", 256, 512),
-    ("lay_fz", 2, 1, "A", 256, 512),
-    ("front", 5),
-    ("q_fz", 2, 0),
-    ("tr_x", 1, 0, "A"),
-    ("lay_gz", 2, "V", 0, 256),
-    ("lay_fz", 2, 1, "V", 0, 256),
-    ("lin", 5),
-    ("lay_al", 1, "A", 256, 512),
-    ("lin", 2),
-    ("tr_gx", 1, 0, "A"),
-    ("mult", 5),
-    ("mult", 2),
-    ("front", 4),
-    ("lay_c", 0, "A", 256, 512),
-    ("q_gz", 2),
-    ("lin", 4),
-    ("q_fz", 2, 1),
+    ("q_fx", 0, 2, 2),
+    ("widen", 1, 2, "A"),
+    ("front", 0),
+    ("widen", 1, 3, "V"),
+    ("widen", 2, 0, "A"),
+    ("widen", 2, 3, "V"),
     ("load_alpha", 2),
-    ("load_fx", 1, 3),
-    ("front", 7),
-    ("lin", 7),
-    ("mult", 4),
-    ("tr_c", 0, 1, "A"),
-    ("front", 6),
-    ("mult", 7),
-    ("tr_c", 0, 0, "A"),
-    ("front", 9),
-    ("lin", 6),
-    ("lin", 9),
-    ("q_gx", 1),
-    ("load_fx", 1, 2),
-    ("lay_al", 1, "A", 0, 256),
-    ("tr_c", 1, 0, "A"),
-    ("mult", 6),
-    ("lay_c", 0, "V", 0, 256),
+    ("front", 1),
+    ("lin", 0),
+    ("lay_gz", 1, "A", 256, 512),
+    ("lay_gz", 1, "G", 0, 256),
+    ("mult", 0),
+    ("front", 3),
+    ("lin", 1),
+    ("front", 2),
+    ("lin", 2),
+    ("mult", 1),
+    ("lay_fz", 2, 1, "A", 256, 512),
+    ("lay_fz", 1, 1, "V", 0, 256),
+    ("lay_fz", 1, 0, "A", 0, 256),
+    ("lin", 3),
+    ("widen", 2, 2, "A"),
+    ("lay_fz", 1, 0, "V", 256, 512),
+    ("q_fz", 1, 1),
+    ("q_gz", 1),
     ("tr_x", 1, 2, "A"),
-    ("front", 8),
-    ("lay_c", 1, "V", 256, 512),
-    ("front", 11),
-    ("lin", 11),
-    ("q_cb", 0, 0, 2),
-    ("mult", 9),
-    ("tr_c", 1, 1, "A"),
-    ("lay_al", 0, "A", 0, 256),
-    ("q_cb", 0, 2, 2),
-    ("tr_x", 1, 3, "A"),
-    ("front", 10),
-    ("lay_al", 2, "A", 256, 512),
-    ("q_fx", 1, 0, 2),
-    ("lin", 8),
-    ("lay_al", 2, "V", 0, 256),
-    ("mult", 11),
-    ("lay_c", 1, "A", 0, 256),
-    ("q_fx", 1, 2, 2),
-    ("mult", 8),
-    ("lin", 12),
-    ("front", 12),
-    ("front", 13),
-    ("lin", 10),
-    ("tr_x", "v", 3, "A"),
-    ("mult", 10),
-    ("q_ca", 1),
-    ("front", 15),
-    ("mult", 12),
-    ("tr_c", 2, 1, "A"),
-    ("lay_al", 0, "A", 256, 512),
-    ("q_ca", 0),
-    ("front", 14),
-    ("tr_c", 2, 0, "A"),
-    ("lin", 13),
-    ("q_al", 2),
-    ("q_al", 1),
-    ("mult", 13),
-    ("tr_x", "v", 0, "A"),
-    ("lay_c", 2, "A", 0, 256),
-    ("q_al", 0),
-    ("front", 17),
     ("load_rows",),
+    ("lay_fz", 2, 1, "V", 0, 256),
+    ("load_gx", 1),
+    ("front", 4),
+    ("tr_x", 1, 0, "A"),
+    ("q_fz", 1, 0),
+    ("q_fz", 2, 1),
+    ("widen", 2, 1, "A"),
+    ("tr_x", 1, 3, "A"),
+    ("lay_gz", 2, "A", 256, 512),
+    ("mult", 2),
+    ("load_alpha", 0),
+    ("mult", 3),
+    ("front", 5),
+    ("front", 7),
+    ("lay_fz", 2, 0, "G", 256, 512),
+    ("lay_gz", 2, "G", 0, 256),
+    ("spread_az", 2),
+    ("lin", 4),
+    ("mult", 4),
+    ("tr_x", 1, 1, "V"),
+    ("tr_c", 0, 1, "A"),
+    ("q_fx", 1, 2, 2),
+    ("lin", 5),
+    ("mult", 5),
+    ("front", 6),
+    ("lay_fz", 2, 0, "G", 0, 256),
+    ("lin", 6),
+    ("tr_gx", 1, 0, "A"),
+    ("q_fx", 1, 0, 2),
+    ("q_gz", 2),
+    ("q_fz", 2, 0),
+    ("lay_c", 0, "A", 256, 512),
+    ("tr_gx", 1, 1, "A"),
+    ("lin", 7),
+    ("mult", 6),
+    ("tr_c", 0, 0, "A"),
+    ("lay_al", 1, "A", 0, 256),
+    ("mult", 7),
+    ("front", 9),
+    ("q_cb", 0, 2, 2),
+    ("q_gx", 1),
+    ("load_v",),
+    ("lin", 9),
+    ("tr_c", 1, 1, "V"),
+    ("tr_x", "v", 2, "A"),
+    ("front", 8),
+    ("lay_c", 0, "G", 0, 256),
+    ("front", 10),
+    ("tr_c", 1, 0, "A"),
+    ("q_ca", 0),
+    ("lay_al", 2, "A", 0, 256),
+    ("mult", 9),
+    ("lin", 8),
+    ("mult", 8),
+    ("lay_c", 1, "G", 256, 512),
+    ("front", 11),
+    ("front", 12),
+    ("lay_c", 1, "A", 0, 256),
+    ("q_cb", 0, 0, 2),
+    ("tr_x", "v", 0, "A"),
+    ("lin", 10),
+    ("q_cb", 1, 0, 2),
+    ("mult", 10),
+    ("lin", 11),
+    ("front", 13),
+    ("mult", 11),
+    ("q_cb", 1, 2, 2),
+    ("lay_al", 0, "G", 256, 512),
+    ("tr_c", 2, 0, "A"),
+    ("lin", 12),
+    ("lay_al", 2, "G", 256, 512),
+    ("lay_al", 0, "G", 0, 256),
+    ("mult", 12),
+    ("front", 15),
+    ("front", 14),
+    ("lay_al", 1, "G", 256, 512),
+    ("lin", 13),
+    ("tr_x", "v", 3, "A"),
+    ("lay_c", 2, "A", 256, 512),
     ("lin", 14),
-    ("q_cb", 2, 0, 2),
+    ("mult", 13),
+    ("front", 18),
     ("lin", 15),
     ("mult", 14),
-    ("lay_c", 2, "A", 256, 512),
-    ("tr_x", "v", 2, "A"),
+    ("q_ca", 1),
+    ("tr_c", 3, 0, "A"),
+    ("lay_c", 2, "G", 0, 256),
     ("mult", 15),
     ("front", 16),
-    ("q_cb", 1, 0, 2),
-    ("front", 19),
-    ("lay_c", 3, "A", 256, 512),
-    ("lay_c", 3, "A", 0, 256),
-    ("lin", 17),
-    ("tr_x", "v", 1, "A"),
-    ("mean_mm", 0, 1),
-    ("q_cb", 1, 2, 2),
+    ("front", 17),
     ("lin", 16),
-    ("q_cb", 2, 2, 2),
-    ("mult", 17),
-    ("mean_out", 0, 1, "V"),
-    ("lin", 19),
+    ("q_cb", 2, 0, 2),
+    ("lin", 17),
+    ("tr_c", 2, 1, "A"),
+    ("q_al", 0),
     ("mult", 16),
-    ("front", 20),
-    ("mean_mm", 0, 2),
-    ("mult", 19),
-    ("front", 18),
-    ("mean_mm", 0, 0),
-    ("q_ca", 2),
-    ("tr_c", 3, 0, "A"),
+    ("tr_x", "v", 1, "A"),
+    ("q_al", 1),
+    ("lay_c", 3, "A", 0, 256),
+    ("mult", 17),
+    ("lay_c", 3, "A", 256, 512),
+    ("q_al", 2),
     ("lin", 18),
-    ("mean_out", 0, 0, "V"),
-    ("mean_out", 0, 2, "V"),
+    ("mult", 18),
+    ("front", 20),
+    ("front", 19),
+    ("lin", 19),
+    ("q_cb", 2, 2, 2),
+    ("mean_mm", 0, 1),
+    ("mean_out", 0, 1, "A"),
+    ("q_ca", 2),
+    ("q_cb", 3, 0, 2),
+    ("tr_c", 3, 1, "A"),
+    ("mean_mm", 0, 0),
+    ("mult", 19),
+    ("lay_c", 4, "A", 0, 256),
+    ("front", 21),
     ("q_ca", 3),
     ("lin", 20),
-    ("mult", 18),
-    ("tr_c", 3, 1, "A"),
-    ("lay_c", 4, "A", 256, 512),
-    ("mult", 20),
+    ("mean_mm", 0, 2),
     ("q_v",),
-    ("tr_c", 4, 1, "A"),
-    ("mean_mm", 0, 3),
+    ("mult", 20),
+    ("mean_out", 0, 0, "A"),
+    ("mean_out", 0, 2, "A"),
     ("tr_c", 4, 0, "A"),
-    ("q_cb", 3, 0, 2),
-    ("lay_c", 4, "A", 0, 256),
-    ("mean_out", 0, 3, "V"),
-    ("q_cb", 3, 2, 2),
+    ("tr_c", 4, 1, "A"),
+    ("lin", 21),
     ("front", 23),
-    ("front", 21),
+    ("front", 22),
+    ("mean_mm", 0, 3),
+    ("mean_out", 0, 3, "V"),
     ("cov_mm", 0, 0),
-    ("cov_out", 0, 0, "V"),
-    ("q_cb", 4, 0, 2),
+    ("cov_out", 0, 0, "A"),
+    ("mult", 21),
+    ("lin", 22),
+    ("q_cb", 4, 2, 2),
+    ("mult", 22),
+    ("lay_c", 4, "A", 256, 512),
+    ("cov_mm", 0, 1),
+    ("cov_out", 0, 1, "V"),
+    ("lin", 23),
+    ("mult", 23),
+    ("cov_mm", 0, 2),
+    ("q_cb", 3, 2, 2),
+    ("tr_c", 5, 0, "A"),
+    ("cov_out", 0, 2, "V"),
+    ("tr_c", 5, 1, "A"),
     ("q_ca", 4),
     ("cov_mm", 0, 3),
-    ("lin", 21),
-    ("mult", 21),
-    ("front", 22),
-    ("lin", 22),
-    ("cov_mm", 1, 1),
-    ("tr_c", 5, 0, "A"),
-    ("cov_out", 0, 3, "V"),
-    ("lin", 23),
-    ("cov_out", 1, 1, "V"),
-    ("cov_mm", 1, 2),
-    ("mult", 22),
-    ("cov_out", 1, 2, "V"),
     ("cov_mm", 1, 0),
-    ("mult", 23),
-    ("mean_mm", 1, 0, (0, 1), "lin"),
-    ("cov_out", 1, 0, "V"),
-    ("cov_mm", 0, 1),
-    ("lay_c", 5, "A", 256, 512),
-    ("q_cb", 5, 0, 2),
-    ("cov_mm", 0, 2),
-    ("mean_mm", 1, 0, (2,)),
-    ("cov_out", 0, 1, "V"),
-    ("cov_out", 0, 2, "V"),
-    ("lay_c", 5, "A", 0, 256),
-    ("mean_mm", 1, 1, (0, 1), "lin"),
-    ("q_cb", 4, 2, 2),
-    ("cov_mm", 1, 3),
-    ("tr_c", 5, 1, "A"),
-    ("mean_out", 1, 0, "V"),
-    ("q_ca", 5),
-    ("cov_out", 1, 3, "V"),
-    ("q_cb", 5, 2, 2),
-    ("mean_mm", 1, 1, (2,)),
-    ("mean_mm", 1, 3, (0, 1), "ex"),
-    ("cov_mm", 2, 2),
-    ("mean_out", 1, 1, "V"),
-    ("cov_mm", 2, 1),
-    ("cov_out", 2, 2, "V"),
-    ("mean_mm", 1, 3, (2,)),
+    ("cov_out", 0, 3, "V"),
     ("mean_mm", 1, 2, (0, 1), "ex"),
-    ("cov_out", 2, 1, "V"),
-    ("mean_out", 1, 3, "V"),
-    ("cov_mm", 2, 0),
+    ("cov_mm", 1, 1),
+    ("cov_out", 1, 0, "V"),
+    ("cov_mm", 1, 2),
+    ("q_cb", 4, 0, 2),
+    ("q_cb", 5, 2, 2),
+    ("cov_out", 1, 1, "V"),
     ("mean_mm", 1, 2, (2,)),
-    ("cov_out", 2, 0, "V"),
+    ("lay_c", 5, "A", 256, 512),
+    ("cov_out", 1, 2, "V"),
+    ("mean_mm", 1, 3, (0, 1), "ex"),
+    ("mean_mm", 1, 3, (2,)),
+    ("cov_mm", 1, 3),
+    ("lay_c", 5, "A", 0, 256),
+    ("q_ca", 5),
+    ("mean_out", 1, 3, "V"),
+    ("cov_out", 1, 3, "V"),
+    ("mean_mm", 1, 1, (0, 1), "lin"),
+    ("cov_mm", 2, 1),
     ("mean_out", 1, 2, "V"),
+    ("cov_out", 2, 1, "V"),
+    ("cov_mm", 2, 2),
+    ("q_cb", 5, 0, 2),
+    ("mean_mm", 1, 0, (0, 1), "lin"),
+    ("mean_mm", 1, 1, (2,)),
+    ("mean_mm", 1, 0, (2,)),
+    ("cov_out", 2, 2, "V"),
     ("cov_mm", 2, 3),
+    ("mean_out", 1, 1, "V"),
+    ("cov_mm", 2, 0),
+    ("mean_out", 1, 0, "V"),
     ("cov_out", 2, 3, "V"),
+    ("cov_out", 2, 0, "V"),
 ]
 
 
@@ -358,34 +348,36 @@ def tile_gp_product_kernel_mean_f6_kernel(
                 store[key] = work.tile(shape, dtype, name=tag, tag=tag, bufs=bufs, align_bytes=64)
             return store[key]
 
-        def load_gx(g, pair):
-            tile_for(gxr, g, [P, 4, D], BF16, "gxr", 2)
-            t = slice(2 * pair, 2 * pair + 2)
-            nc.sync.dma_start(out=gxr[g][:, t], in_=gx_v[g][:, t])
+        def load_gx(g):
+            tile_for(gxr, g, [P, 4, D], BF16, "rows4", 4)
+            nc.sync.dma_start(out=gxr[g][:], in_=gx_v[g])
 
         def load_fz(h, s):
-            tile_for(fzr, h, [P, S, 4, B], BF16, "fzr", 3)
-            nc.sync.dma_start(out=fzr[h][:, s], in_=fz_v[s][:, :, h * B : (h + 1) * B])
+            if h == 0:
+                tile_for(fzr, 0, [P, S, 4, B], BF16, "fza", 1)
+                nc.sync.dma_start(out=fzr[0][:, s], in_=fz_v[s][:, :, 0:B])
+            else:
+                tile_for(fzr, 1, [P, S, 4, N - B], BF16, "fzb", 1)
+                nc.sync.dma_start(out=fzr[1][:, s], in_=fz_v[s][:, :, B:N])
 
-        def load_fx(g, t):
+        def load_fx(g, t, n):
             tile_for(xr, g, [P, 4, K], BF16, "xr", 2)
-            nc.sync.dma_start(out=xr[g][:, t], in_=fx_v[g][:, t])
+            nc.sync.dma_start(out=xr[g][:, t : t + n], in_=fx_v[g][:, t : t + n])
 
-        gzb = {}
+        gzb = [keep.tile([P, 4, B], U8, name="gzb0"), keep.tile([P, 4, N - B], U8, name="gzb1")]
 
         def load_gz(h):
-            gzb[h] = keep.tile([P, 4, B], U8, name="gzb%d" % h)
-            nc.sync.dma_start(out=gzb[h][:], in_=gz_v[:, :, h * B : (h + 1) * B])
+            nc.sync.dma_start(out=gzb[h][:], in_=gz_v[:, :, 0:B] if h == 0 else gz_v[:, :, B:N])
 
         def load_alpha(h):
-            alr[h] = work.tile([P, 4, R], BF16, name="alr", tag="alr", bufs=3, align_bytes=64)
+            tile_for(alr, h, [P, 4, R], BF16, "rows4", 4)
             nc.sync.dma_start(out=alr[h][:], in_=al_v[h])
 
         prec_b = keep.tile([P, N], BF16, name="prec_b", align_bytes=64)
         prior_b = keep.tile([P, R], BF16, name="prior_b", align_bytes=64)
 
         def load_v():
-            xr["v"] = work.tile([P, 4, M], BF16, name="xr", tag="xr", bufs=2, align_bytes=64)
+            tile_for(xr, "v", [P, 4, M], BF16, "xr", 2)
             nc.sync.dma_start(out=xr["v"][:], in_=v_v)
 
         def load_rows():
@@ -405,6 +397,9 @@ def tile_gp_product_kernel_mean_f6_kernel(
                 nc.vector.tensor_copy(out=out, in_=in_)
             else:
                 nc.gpsimd.tensor_scalar(out=out, in0=in_, scalar1=1.0, scalar2=0.0, op0=ALU.mult, op1=ALU.add)
+
+        def interleave(eng, out, in_):
+            copy_on(eng, out.rearrange("p (c i) j -> p c j i", i=4), in_.rearrange("p j (c i) -> p c j i", i=4))
 
         def spread_az(h):
             bank = psum.tile([P, B], F32, name="acc", tag="acc", bufs=2)
@@ -445,14 +440,14 @@ def tile_gp_product_kernel_mean_f6_kernel(
             return mix[key]
 
         def lay(key, src, eng, a=0, b=B):
-            copy_on(eng, mixed(key)[:, a:b, :], src[:, :, a:b].rearrange("p j n -> p n j"))
+            interleave(eng, mixed(key)[:, a:b, :], src[:, :, a:b])
 
         def q_lay(dst, first, key):
             quantize(dst, first, mix[key][:].rearrange("p n j -> p (n j)"))
 
         def widen(h, j, eng="A"):
             tile_for(gzw, h, [P, 4, B], BF16, "gzw", 2)
-            src = gzb[h][:, j, :].bitcast(FP8)
+            src = (gzb[0][:, j, :] if h == 0 else gzb[1][:, j, (h - 1) * B : h * B]).bitcast(FP8)
             if eng == "V":
                 nc.vector.tensor_scalar(out=gzw[h][:, j, :], in0=src, scalar1=gzs[:, j : j + 1], scalar2=None, op0=ALU.mult)
             else:
@@ -465,7 +460,8 @@ def tile_gp_product_kernel_mean_f6_kernel(
             q_lay(gz_q, h * B, ("gz", h))
 
         def lay_fz(h, s, eng, a=0, b=B):
-            lay(("fz", h, s), fzr[h][:, s], eng, a, b)
+            raw = fzr[0][:, s] if h == 0 else fzr[1][:, s, :, (h - 1) * B : h * B]
+            lay(("fz", h, s), raw, eng, a, b)
 
         def q_fz(h, s):
             q_lay(fz_q, (h * S + s) * B, ("fz", h, s))
@@ -518,7 +514,7 @@ def tile_gp_product_kernel_mean_f6_kernel(
         def lay_c(k, eng, a=0, b=B):
             if k not in cag:
                 cag[k] = work.tile([P, B, 4], BF16, name="cag", tag="cag", bufs=2, align_bytes=64)
-            copy_on(eng, cag[k][:, a:b, :], c_nat[k][:, :, a:b].rearrange("p t n -> p n t"))
+            interleave(eng, cag[k][:, a:b, :], c_nat[k][:, :, a:b])
 
         def q_ca(k):
             quantize(ca_q, k * B, cag[k][:].rearrange("p n t -> p (n t)"))
@@ -539,7 +535,8 @@ def tile_gp_product_kernel_mean_f6_kernel(
         res = {}
 
         def result(key, i):
-            return tile_for(res, key, [P, 4, B], F32, "fzr", 3)[:, i, :]
+            tag = "fza" if key in (("mean", 0), ("cov", 1)) else "xr"
+            return tile_for(res, key, [P, 4, B], F32, tag, 1 if tag == "fza" else 2)[:, i, :]
 
         def cov_out(h, b, eng="V"):
             o = result(("cov", h), b)

from contextlib import ExitStack

import concourse.mybir as mybir
from concourse.masks import make_identity

M, N, K, D, R, Q = 1024, 1536, 1024, 512, 512, 512
FLOPS = 2 * M * N * (K + D + R + Q)

F32 = mybir.dt.float32
BF16 = mybir.dt.bfloat16
U32 = mybir.dt.uint32
I32 = mybir.dt.int32
U8 = mybir.dt.uint8
FP8 = mybir.dt.float8_e4m3fn
FP8X4 = mybir.dt.float8_e4m3fn_x4
ACT = mybir.ActivationFunctionType
ALU = mybir.AluOpType

P = 128
B = 512


SEQ = [
    ("load_gz", 0),
    ("load_fz", 0, 0),
    ("widen", 0, 1, "V"),
    ("widen", 0, 2, "V"),
    ("widen", 0, 0, "V"),
    ("load_fx", 0, 0, 2),
    ("lay_fz", 0, 0, "V", 256, 512),
    ("load_gx", 0),
    ("widen", 0, 3, "V"),
    ("lay_fz", 0, 0, "V", 0, 256),
    ("spread_az", 0),
    ("load_fz", 0, 1),
    ("lay_gz", 0, "A", 0, 256),
    ("q_fz", 0, 0),
    ("tr_x", 0, 0, "A"),
    ("lay_gz", 0, "V", 256, 512),
    ("load_fx", 0, 2, 2),
    ("tr_x", 0, 1, "A"),
    ("spread_az", 1),
    ("q_gz", 0),
    ("load_gz", 1),
    ("load_fz", 1, 1),
    ("tr_gx", 0, 0, "A"),
    ("load_fz", 1, 0),
    ("lay_fz", 0, 1, "V", 0, 256),
    ("lay_fz", 0, 1, "V", 256, 512),
    ("q_fx", 0, 0, 1),
    ("tr_gx", 0, 1, "A"),
    ("tr_x", 0, 3, "A"),
    ("tr_x", 0, 2, "A"),
    ("widen", 1, 1, "A"),
    ("lay_fz", 1, 1, "G", 256, 512),
    ("widen", 1, 0, "A"),
    ("load_fx", 1, 0, 4),
    ("q_fz", 0, 1),
    ("q_gx", 0),
    ("q_fx", 0, 1, 1),
    ("load_alpha", 1),
    ("q_fx", 0, 2, 2),
    ("widen", 1, 2, "A"),
    ("front", 0),
    ("widen", 1, 3, "V"),
    ("widen", 2, 0, "A"),
    ("widen", 2, 3, "V"),
    ("load_alpha", 2),
    ("front", 1),
    ("lin", 0),
    ("lay_gz", 1, "A", 256, 512),
    ("lay_gz", 1, "G", 0, 256),
    ("mult", 0),
    ("front", 3),
    ("lin", 1),
    ("front", 2),
    ("lin", 2),
    ("mult", 1),
    ("lay_fz", 2, 1, "A", 256, 512),
    ("lay_fz", 1, 1, "V", 0, 256),
    ("lay_fz", 1, 0, "A", 0, 256),
    ("lin", 3),
    ("widen", 2, 2, "A"),
    ("lay_fz", 1, 0, "V", 256, 512),
    ("q_fz", 1, 1),
    ("q_gz", 1),
    ("tr_x", 1, 2, "A"),
    ("load_rows",),
    ("lay_fz", 2, 1, "V", 0, 256),
    ("load_gx", 1),
    ("front", 4),
    ("tr_x", 1, 0, "A"),
    ("q_fz", 1, 0),
    ("q_fz", 2, 1),
    ("widen", 2, 1, "A"),
    ("tr_x", 1, 3, "A"),
    ("lay_gz", 2, "A", 256, 512),
    ("mult", 2),
    ("load_alpha", 0),
    ("mult", 3),
    ("front", 5),
    ("front", 7),
    ("lay_fz", 2, 0, "G", 256, 512),
    ("lay_gz", 2, "G", 0, 256),
    ("spread_az", 2),
    ("lin", 4),
    ("mult", 4),
    ("tr_x", 1, 1, "V"),
    ("tr_c", 0, 1, "A"),
    ("q_fx", 1, 2, 2),
    ("lin", 5),
    ("mult", 5),
    ("front", 6),
    ("lay_fz", 2, 0, "G", 0, 256),
    ("lin", 6),
    ("tr_gx", 1, 0, "A"),
    ("q_fx", 1, 0, 2),
    ("q_gz", 2),
    ("q_fz", 2, 0),
    ("lay_c", 0, "A", 256, 512),
    ("tr_gx", 1, 1, "A"),
    ("lin", 7),
    ("mult", 6),
    ("tr_c", 0, 0, "A"),
    ("lay_al", 1, "A", 0, 256),
    ("mult", 7),
    ("front", 9),
    ("q_cb", 0, 2, 2),
    ("q_gx", 1),
    ("load_v",),
    ("lin", 9),
    ("tr_c", 1, 1, "V"),
    ("tr_x", "v", 2, "A"),
    ("front", 8),
    ("lay_c", 0, "G", 0, 256),
    ("front", 10),
    ("tr_c", 1, 0, "A"),
    ("q_ca", 0),
    ("lay_al", 2, "A", 0, 256),
    ("mult", 9),
    ("lin", 8),
    ("mult", 8),
    ("lay_c", 1, "G", 256, 512),
    ("front", 11),
    ("front", 12),
    ("lay_c", 1, "A", 0, 256),
    ("q_cb", 0, 0, 2),
    ("tr_x", "v", 0, "A"),
    ("lin", 10),
    ("q_cb", 1, 0, 2),
    ("mult", 10),
    ("lin", 11),
    ("front", 13),
    ("mult", 11),
    ("q_cb", 1, 2, 2),
    ("lay_al", 0, "G", 256, 512),
    ("tr_c", 2, 0, "A"),
    ("lin", 12),
    ("lay_al", 2, "G", 256, 512),
    ("lay_al", 0, "G", 0, 256),
    ("mult", 12),
    ("front", 15),
    ("front", 14),
    ("lay_al", 1, "G", 256, 512),
    ("lin", 13),
    ("tr_x", "v", 3, "A"),
    ("lay_c", 2, "A", 256, 512),
    ("lin", 14),
    ("mult", 13),
    ("front", 18),
    ("lin", 15),
    ("mult", 14),
    ("q_ca", 1),
    ("tr_c", 3, 0, "A"),
    ("lay_c", 2, "G", 0, 256),
    ("mult", 15),
    ("front", 16),
    ("front", 17),
    ("lin", 16),
    ("q_cb", 2, 0, 2),
    ("lin", 17),
    ("tr_c", 2, 1, "A"),
    ("q_al", 0),
    ("mult", 16),
    ("tr_x", "v", 1, "A"),
    ("q_al", 1),
    ("lay_c", 3, "A", 0, 256),
    ("mult", 17),
    ("lay_c", 3, "A", 256, 512),
    ("q_al", 2),
    ("lin", 18),
    ("mult", 18),
    ("front", 20),
    ("front", 19),
    ("lin", 19),
    ("q_cb", 2, 2, 2),
    ("mean_mm", 0, 1),
    ("mean_out", 0, 1, "A"),
    ("q_ca", 2),
    ("q_cb", 3, 0, 2),
    ("tr_c", 3, 1, "A"),
    ("mean_mm", 0, 0),
    ("mult", 19),
    ("lay_c", 4, "A", 0, 256),
    ("front", 21),
    ("q_ca", 3),
    ("lin", 20),
    ("mean_mm", 0, 2),
    ("q_v",),
    ("mult", 20),
    ("mean_out", 0, 0, "A"),
    ("mean_out", 0, 2, "A"),
    ("tr_c", 4, 0, "A"),
    ("tr_c", 4, 1, "A"),
    ("lin", 21),
    ("front", 23),
    ("front", 22),
    ("mean_mm", 0, 3),
    ("mean_out", 0, 3, "V"),
    ("cov_mm", 0, 0),
    ("cov_out", 0, 0, "A"),
    ("mult", 21),
    ("lin", 22),
    ("q_cb", 4, 2, 2),
    ("mult", 22),
    ("lay_c", 4, "A", 256, 512),
    ("cov_mm", 0, 1),
    ("cov_out", 0, 1, "V"),
    ("lin", 23),
    ("mult", 23),
    ("cov_mm", 0, 2),
    ("q_cb", 3, 2, 2),
    ("tr_c", 5, 0, "A"),
    ("cov_out", 0, 2, "V"),
    ("tr_c", 5, 1, "A"),
    ("q_ca", 4),
    ("cov_mm", 0, 3),
    ("cov_mm", 1, 0),
    ("cov_out", 0, 3, "V"),
    ("mean_mm", 1, 2, (0, 1), "ex"),
    ("cov_mm", 1, 1),
    ("cov_out", 1, 0, "V"),
    ("cov_mm", 1, 2),
    ("q_cb", 4, 0, 2),
    ("q_cb", 5, 2, 2),
    ("cov_out", 1, 1, "V"),
    ("mean_mm", 1, 2, (2,)),
    ("lay_c", 5, "A", 256, 512),
    ("cov_out", 1, 2, "V"),
    ("mean_mm", 1, 3, (0, 1), "ex"),
    ("mean_mm", 1, 3, (2,)),
    ("cov_mm", 1, 3),
    ("lay_c", 5, "A", 0, 256),
    ("q_ca", 5),
    ("mean_out", 1, 3, "V"),
    ("cov_out", 1, 3, "V"),
    ("mean_mm", 1, 1, (0, 1), "lin"),
    ("cov_mm", 2, 1),
    ("mean_out", 1, 2, "V"),
    ("cov_out", 2, 1, "V"),
    ("cov_mm", 2, 2),
    ("q_cb", 5, 0, 2),
    ("mean_mm", 1, 0, (0, 1), "lin"),
    ("mean_mm", 1, 1, (2,)),
    ("mean_mm", 1, 0, (2,)),
    ("cov_out", 2, 2, "V"),
    ("cov_mm", 2, 3),
    ("mean_out", 1, 1, "V"),
    ("cov_mm", 2, 0),
    ("mean_out", 1, 0, "V"),
    ("cov_out", 2, 3, "V"),
    ("cov_out", 2, 0, "V"),
]


def tile_gp_product_kernel_mean_f6_kernel(
    tc, fx, fz, gx, gz_bytes, gz_scale, amp_x, amp_z, alpha, prior, scale_x, v, prec_z, out_0, out_1
):
    nc = tc.nc
    G, H, S = M // B, N // B, K // B

    with ExitStack() as ctx:
        keep = ctx.enter_context(tc.tile_pool(name="keep", bufs=1))
        work = ctx.enter_context(tc.tile_pool(name="work", bufs=2))
        psum = ctx.enter_context(tc.psum_pool(name="psum", bufs=2))
        ctx.enter_context(tc.manual_schedule())

        def codes_and_scales(name, words):
            codes = keep.tile([P, words], U32, name=name + "_codes", align_bytes=256)
            scales = keep.tile([P, words], U8, name=name + "_scales", align_bytes=256)
            return codes, scales

        fx_q = codes_and_scales("fx", S * M)
        fz_q = codes_and_scales("fz", S * N)
        gx_q = codes_and_scales("gx", M)
        gz_q = codes_and_scales("gz", N)
        al_q = codes_and_scales("al", H * R)
        v_q = codes_and_scales("v", G * Q)
        ca_q = codes_and_scales("ca", G * N)
        cb_q = codes_and_scales("cb", H * M)

        def quantize(dst, first, in_):
            codes, scales = dst
            width = in_.shape[1] // 4
            cols = slice(first, first + width)
            nc.vector.quantize_mx(out=codes[:, cols].bitcast(FP8X4), scales=scales[:, cols], in_=in_)

        def mm(out, lhs, l0, rhs, r0, start, stop):
            nc.tensor.matmul_mx(
                out=out,
                lhsT=lhs[0][:, l0 : l0 + P].bitcast(FP8X4),
                lhsT_scale=lhs[1][:, l0 : l0 + P],
                rhs=rhs[0][:, r0 : r0 + B].bitcast(FP8X4),
                rhs_scale=rhs[1][:, r0 : r0 + B],
                start=start,
                stop=stop,
            )

        warm = keep.tile([P, 1], F32, name="warm")
        nc.gpsimd.memset(warm[:], 0.0)
        az_rows = keep.tile([P, N], BF16, name="az_rows", align_bytes=64)
        nc.gpsimd.memset(az_rows[:].bitcast(I32), 0)
        ident = keep.tile([P, P], F32, name="ident")
        make_identity(nc, ident[:])
        ones = keep.tile([P, P], BF16, name="ones")
        nc.gpsimd.memset(ones[:], 1.0)
        warm2 = keep.tile([P, 1], F32, name="warm2")
        nc.scalar.activation(out=warm2[:], in_=warm[:], func=ACT.Exp)

        gzs = keep.tile([P, 4], F32, name="gzs")
        nc.scalar.dma_start(out=gzs[:], in_=gz_scale.rearrange("(p j) o -> p (j o)", j=4))
        ax16 = keep.tile([P, G, 4], BF16, name="ax16")
        nc.scalar.dma_start(out=ax16[:], in_=amp_x.rearrange("(g p t) -> p g t", p=P, t=4))
        sx16 = keep.tile([P, G, 4], BF16, name="sx16")
        nc.scalar.dma_start(out=sx16[:], in_=scale_x.rearrange("(g p t) -> p g t", p=P, t=4))
        nc.scalar.dma_start(out=az_rows[0:1, :], in_=amp_z.rearrange("(o n) -> o n", o=1))

        gz_v = gz_bytes.rearrange("(p j) n -> p j n", j=4)
        fz_v = fz.rearrange("(s p j) n -> s p j n", p=P, j=4)
        fx_v = fx.rearrange("(g p t) k -> g p t k", p=P, t=4)
        gx_v = gx.rearrange("(g p t) d -> g p t d", p=P, t=4)
        al_v = alpha.rearrange("(h p j) r -> h p j r", p=P, j=4)
        v_v = v.rearrange("(p b) m -> p b m", b=4)
        gxr, fzr, xr, alr = {}, {}, {}, {}

        def tile_for(store, key, shape, dtype, tag, bufs):
            if key not in store:
                store[key] = work.tile(shape, dtype, name=tag, tag=tag, bufs=bufs, align_bytes=64)
            return store[key]

        def load_gx(g):
            tile_for(gxr, g, [P, 4, D], BF16, "rows4", 4)
            nc.sync.dma_start(out=gxr[g][:], in_=gx_v[g])

        def load_fz(h, s):
            if h == 0:
                tile_for(fzr, 0, [P, S, 4, B], BF16, "fza", 1)
                nc.sync.dma_start(out=fzr[0][:, s], in_=fz_v[s][:, :, 0:B])
            else:
                tile_for(fzr, 1, [P, S, 4, N - B], BF16, "fzb", 1)
                nc.sync.dma_start(out=fzr[1][:, s], in_=fz_v[s][:, :, B:N])

        def load_fx(g, t, n):
            tile_for(xr, g, [P, 4, K], BF16, "xr", 2)
            nc.sync.dma_start(out=xr[g][:, t : t + n], in_=fx_v[g][:, t : t + n])

        gzb = [keep.tile([P, 4, B], U8, name="gzb0"), keep.tile([P, 4, N - B], U8, name="gzb1")]

        def load_gz(h):
            nc.sync.dma_start(out=gzb[h][:], in_=gz_v[:, :, 0:B] if h == 0 else gz_v[:, :, B:N])

        def load_alpha(h):
            tile_for(alr, h, [P, 4, R], BF16, "rows4", 4)
            nc.sync.dma_start(out=alr[h][:], in_=al_v[h])

        prec_b = keep.tile([P, N], BF16, name="prec_b", align_bytes=64)
        prior_b = keep.tile([P, R], BF16, name="prior_b", align_bytes=64)

        def load_v():
            tile_for(xr, "v", [P, 4, M], BF16, "xr", 2)
            nc.sync.dma_start(out=xr["v"][:], in_=v_v)

        def load_rows():
            nc.sync.dma_start(out=prior_b[:], in_=prior.partition_broadcast(P))
            nc.sync.dma_start(out=prec_b[:], in_=prec_z.partition_broadcast(P))

        ax = keep.tile([P, G, 4], F32, name="ax")
        nc.gpsimd.tensor_copy(out=ax[:], in_=ax16[:])
        sx = keep.tile([P, G, 4], F32, name="sx")
        nc.gpsimd.tensor_copy(out=sx[:], in_=sx16[:])
        az_b = keep.tile([P, N], BF16, name="az_b", align_bytes=64)

        def copy_on(eng, out, in_):
            if eng == "A":
                nc.scalar.copy(out=out, in_=in_)
            elif eng == "V":
                nc.vector.tensor_copy(out=out, in_=in_)
            else:
                nc.gpsimd.tensor_scalar(out=out, in0=in_, scalar1=1.0, scalar2=0.0, op0=ALU.mult, op1=ALU.add)

        def interleave(eng, out, in_):
            copy_on(eng, out.rearrange("p (c i) j -> p c j i", i=4), in_.rearrange("p j (c i) -> p c j i", i=4))

        def spread_az(h):
            bank = psum.tile([P, B], F32, name="acc", tag="acc", bufs=2)
            nc.tensor.matmul(out=bank[:], lhsT=ones[:], rhs=az_rows[:, h * B : (h + 1) * B], start=True, stop=True)
            nc.scalar.copy(out=az_b[:, h * B : (h + 1) * B], in_=bank[:])

        def turn(words, firsts, grouped, eng="A"):
            bank = psum.tile([P, 4, P], F32, name="tr", tag="tr", bufs=2)
            for i in range(4):
                nc.tensor.transpose(bank[:, i, :], words[i // 2][:, firsts[i // 2] + i % 2 : firsts[i // 2] + 256 : 2], ident[:])
            out = grouped.rearrange("p a m j -> p a (m j)").bitcast(F32).rearrange("p a (m u) -> p a m u", u=2)
            copy_on(eng, out, bank[:].rearrange("p (a u) m -> p a m u", u=2))

        gxg, xg, mix, gzw = {}, {}, {}, {}

        def tr_gx(g, pair, eng="A"):
            tile_for(gxg, g, [P, 4, P, 4], BF16, "mix", 4)
            words = [gxr[g][:, 2 * pair + i, :].bitcast(F32) for i in range(2)]
            turn(words, (0, 0), gxg[g][:, 2 * pair : 2 * pair + 2], eng)

        def q_gx(g):
            quantize(gx_q, g * B, gxg[g][:].rearrange("p t m j -> p (t m j)"))

        def tr_x(g, t, eng="A"):
            tile_for(xg, g, [P, 4, S, P, 4], BF16, "xg", 1)
            words = xr[g][:, t, :].bitcast(F32)
            turn([words, words], (0, 256), xg[g][:, t], eng)

        def q_fx(g, t0, n):
            quantize(fx_q, (g * 4 + t0) * S * P, xg[g][:, t0 : t0 + n].rearrange("p t s m j -> p (t s m j)"))

        def q_v():
            quantize(v_q, 0, xg["v"][:].rearrange("p t s m j -> p (t s m j)"))

        def mixed(key):
            if key not in mix:
                mix[key] = work.tile([P, B, 4], BF16, name="mix", tag="mix", bufs=4, align_bytes=64)
            return mix[key]

        def lay(key, src, eng, a=0, b=B):
            interleave(eng, mixed(key)[:, a:b, :], src[:, :, a:b])

        def q_lay(dst, first, key):
            quantize(dst, first, mix[key][:].rearrange("p n j -> p (n j)"))

        def widen(h, j, eng="A"):
            tile_for(gzw, h, [P, 4, B], BF16, "gzw", 2)
            src = (gzb[0][:, j, :] if h == 0 else gzb[1][:, j, (h - 1) * B : h * B]).bitcast(FP8)
            if eng == "V":
                nc.vector.tensor_scalar(out=gzw[h][:, j, :], in0=src, scalar1=gzs[:, j : j + 1], scalar2=None, op0=ALU.mult)
            else:
                nc.scalar.activation(out=gzw[h][:, j, :], in_=src, func=ACT.Copy, scale=gzs[:, j : j + 1])

        def lay_gz(h, eng, a=0, b=B):
            lay(("gz", h), gzw[h], eng, a, b)

        def q_gz(h):
            q_lay(gz_q, h * B, ("gz", h))

        def lay_fz(h, s, eng, a=0, b=B):
            raw = fzr[0][:, s] if h == 0 else fzr[1][:, s, :, (h - 1) * B : h * B]
            lay(("fz", h, s), raw, eng, a, b)

        def q_fz(h, s):
            q_lay(fz_q, (h * S + s) * B, ("fz", h, s))

        def lay_al(h, eng, a=0, b=B):
            lay(("al", h), alr[h], eng, a, b)

        def q_al(h):
            q_lay(al_q, h * R, ("al", h))

        ex_b, lin_b, x_t, e_t, c_nat, cag, cbg = {}, {}, {}, {}, {}, {}, {}

        def where(i):
            k, t = i // 4, i % 4
            return k // H, k % H, t

        def front(i):
            g, h, t = where(i)
            ex_b[i] = psum.tile([P, B], F32, name="ex", tag="ex", bufs=2)
            mm(ex_b[i][:], gx_q, (g * 4 + t) * P, gz_q, h * B, True, True)
            add(i)
            exp(i)

        def lin(i):
            g, h, t = where(i)
            lin_b[i] = psum.tile([P, B], F32, name="lin", tag="lin", bufs=2)
            for s in range(S):
                mm(lin_b[i][:], fx_q, ((g * 4 + t) * S + s) * P, fz_q, (h * S + s) * B, s == 0, s == S - 1)

        def add(i):
            g, h, t = where(i)
            x_t[i] = work.tile([P, B], F32, name="xt", tag="xt", bufs=2)
            nc.vector.tensor_tensor(out=x_t[i][:], in0=ex_b[i][:], in1=az_b[:, h * B : (h + 1) * B], op=ALU.add)

        def exp(i):
            g, h, t = where(i)
            e_t[i] = work.tile([P, B], F32, name="et", tag="et", bufs=3)
            nc.scalar.activation(out=e_t[i][:], in_=x_t[i][:], func=ACT.Exp, bias=ax[:, g, t : t + 1])

        def mult(i):
            k, t = i // 4, i % 4
            tile_for(c_nat, k, [P, 4, B], BF16, "cnat", 2)
            nc.vector.tensor_tensor(out=c_nat[k][:, t, :], in0=lin_b[i][:], in1=e_t[i][:], op=ALU.mult)

        def tr_c(k, pair, eng="A"):
            tile_for(cbg, k, [P, 4, P, 4], BF16, "cbg", 2)
            words = [c_nat[k][:, 2 * pair + i, :].bitcast(F32) for i in range(2)]
            turn(words, (0, 0), cbg[k][:, 2 * pair : 2 * pair + 2], eng)

        def lay_c(k, eng, a=0, b=B):
            if k not in cag:
                cag[k] = work.tile([P, B, 4], BF16, name="cag", tag="cag", bufs=2, align_bytes=64)
            interleave(eng, cag[k][:, a:b, :], c_nat[k][:, :, a:b])

        def q_ca(k):
            quantize(ca_q, k * B, cag[k][:].rearrange("p n t -> p (n t)"))

        def q_cb(k, t0=0, n=4):
            g, h = k // H, k % H
            quantize(cb_q, (h * G + g) * B + t0 * P, cbg[k][:, t0 : t0 + n].rearrange("p t m j -> p (t m j)"))

        acc = {}
        cov_v = out_1.rearrange("(p b) n -> b p n", b=4)
        mean_v = out_0.rearrange("(g p t) r -> g t p r", p=P, t=4)

        def cov_mm(h, b, tag="acc"):
            acc["cov", h, b] = psum.tile([P, B], F32, name=tag, tag=tag, bufs=2)
            for g in range(G):
                mm(acc["cov", h, b][:], v_q, (b * G + g) * P, ca_q, (g * H + h) * B, g == 0, g == G - 1)

        res = {}

        def result(key, i):
            tag = "fza" if key in (("mean", 0), ("cov", 1)) else "xr"
            return tile_for(res, key, [P, 4, B], F32, tag, 1 if tag == "fza" else 2)[:, i, :]

        def cov_out(h, b, eng="V"):
            o = result(("cov", h), b)
            if eng == "V":
                nc.vector.tensor_tensor(out=o, in0=acc["cov", h, b][:], in1=prec_b[:, h * B : (h + 1) * B], op=ALU.mult)
            else:
                m = work.tile([P, B], F32, name="mid", tag="mid", bufs=2)
                nc.scalar.copy(out=m[:], in_=acc["cov", h, b][:])
                nc.gpsimd.tensor_tensor(out=o, in0=m[:], in1=prec_b[:, h * B : (h + 1) * B], op=ALU.mult)
            nc.sync.dma_start(out=cov_v[b][:, h * B : (h + 1) * B], in_=o)

        def mean_mm(g, t, hs=(0, 1, 2), tag="acc"):
            if hs[0] == 0:
                acc["mean", g, t] = psum.tile([P, R], F32, name=tag, tag=tag, bufs=2)
            for h in hs:
                mm(acc["mean", g, t][:], cb_q, (h * G + g) * B + t * P, al_q, h * R, h == 0, h == H - 1)

        def mean_out(g, t, eng="V"):
            o = result(("mean", g), t)
            if eng == "V":
                nc.vector.scalar_tensor_tensor(
                    out=o, in0=acc["mean", g, t][:], scalar=sx[:, g, t : t + 1], in1=prior_b[:], op0=ALU.mult, op1=ALU.add
                )
            else:
                m = work.tile([P, B], F32, name="mid", tag="mid", bufs=2)
                nc.scalar.activation(out=m[:], in_=acc["mean", g, t][:], func=ACT.Copy, scale=sx[:, g, t : t + 1])
                nc.gpsimd.tensor_tensor(out=o, in0=m[:], in1=prior_b[:], op=ALU.add)
            nc.sync.dma_start(out=mean_v[g, t], in_=o)

        ops = dict(
            widen=widen, tr_gx=tr_gx, tr_x=tr_x, lay_gz=lay_gz, lay_fz=lay_fz, lay_al=lay_al, lay_c=lay_c, q_gx=q_gx, q_fx=q_fx,
            q_v=q_v, q_gz=q_gz, q_fz=q_fz, q_al=q_al, q_ca=q_ca, q_cb=q_cb, spread_az=spread_az, front=front, lin=lin, mult=mult,
            tr_c=tr_c, cov_mm=cov_mm, cov_out=cov_out, mean_mm=mean_mm, mean_out=mean_out, load_gx=load_gx, load_fz=load_fz, load_fx=load_fx, load_gz=load_gz,
            load_alpha=load_alpha, load_v=load_v, load_rows=load_rows,
        )
        for name, *args in SEQ:
            ops[name](*args)
